import numpy as np
import ml_dtypes


def mxq(x, axis, fmt="e4m3"):
    dtype, down = {"e4m3": (ml_dtypes.float8_e4m3fn, 7), "e5m2": (ml_dtypes.float8_e5m2, 14)}[fmt]
    v = np.moveaxis(np.asarray(x, np.float32).astype(ml_dtypes.bfloat16).astype(np.float64), axis, -1)
    blocks = v.reshape(v.shape[:-1] + (-1, 32))
    amax = np.abs(blocks).max(-1, keepdims=True)
    byte = np.maximum(np.where(amax > 0, np.frexp(amax)[1] - 1 + 127, 0) - down, 1)
    scale = np.exp2(byte - 127.0)
    codes = (blocks / scale).astype(np.float32).astype(dtype).astype(np.float64)
    return np.moveaxis((codes * scale).reshape(v.shape), -1, axis)


WIDE = False


def mx_kscale(k):
    if not WIDE:
        return np.ones(k)
    levels = np.array([18, -18])
    if k % 512:
        return np.exp2(np.random.permutation(np.resize(levels, k // 32))).repeat(32)
    a = np.empty((k // 512, 16))
    for p in range(k // 512):
        a[p, :8] = np.random.permutation(np.resize(levels, 8))
        for g in range(8):
            far = levels[np.abs(levels - a[p, g]) >= 10]
            a[p, g + 8] = far[np.random.randint(len(far))]
    return np.exp2(a.ravel()).repeat(32)


def f64(x):
    return np.asarray(x).astype(np.float64)


def striped(idx):
    return np.tile(np.asarray(idx).reshape(-1, 16).T, (8, 1)).astype(np.uint16)


def unstriped(offs):
    return offs[:16].T.reshape(-1).astype(np.int64)


def eight(idx):
    return np.concatenate([idx[h].reshape(-1, 16).T for h in range(8)]).astype(np.uint16)


def uneight(offs):
    return np.stack([offs[16 * h:16 * h + 16].T.reshape(-1) for h in range(8)]).astype(np.int64)


def setup_inputs():
    n = np.random.standard_normal
    uni = np.random.uniform
    idx = np.stack([np.random.permutation(2048)[:512] for _ in range(8)])
    soft_y = np.exp(0.4 * n((512, 512)))
    f_d = mx_kscale(512)
    f_r = mx_kscale(512)
    return {
        "xT": (0.35 * n((512, 512)) * f_d[:, None] * f_r[None, :]).astype(np.float32),
        "mT": (n((512, 2048)) / np.sqrt(512) / f_d[:, None]).astype(np.float32),
        "us": (uni(0.75, 1.3, (512, 1)) / f_r[:, None]).astype(np.float32),
        "wt": (uni(0.75, 1.3, (512, 1))).astype(np.float32),
        "te": np.tile(uni(0.75, 1.3, 512), (128, 1)).astype(np.float32),
        "y": (soft_y / soft_y.sum(-1, keepdims=True)).astype(np.float32),
        "offs": eight(idx),
    }


def reference(xT, mT, us, wt, te, y, offs):
    idx = uneight(offs)
    mT_i = np.concatenate([f64(mT)[64 * run:64 * run + 64][:, idx[run % 8]] for run in range(8)])
    a = mxq(f64(xT), 0, "e4m3").T @ mxq(mT_i, 0, "e4m3")
    z = f64(us) * f64(te)[:1] * a
    m = (z).max(-1, keepdims=True)
    e = np.exp(z - m)
    tot = (e).sum(-1, keepdims=True)
    g = f64(wt) * f64(us) * f64(te)[:1] * (e / tot - f64(y))
    dw = mxq(f64(xT), 1, "e4m3") @ mxq(g, 0, "e5m2")
    out = np.zeros((512, 2048))
    for run in range(8):
        out[64 * run:64 * run + 64][:, idx[run % 8]] = dw[64 * run:64 * run + 64]
    return out

@@ -1,0 +1,224 @@
+from contextlib import ExitStack
+
+import concourse.mybir as mybir
+from concourse.masks import make_identity
+
+D, R, ENTRIES, PLACES = 512, 512, 512, 2048
+FLOPS = 2 * 2 * D * R * ENTRIES
+
+F32 = mybir.dt.float32
+BF16 = mybir.dt.bfloat16
+U32 = mybir.dt.uint32
+U16 = mybir.dt.uint16
+U8 = mybir.dt.uint8
+E4M3X4 = mybir.dt.float8_e4m3fn_x4
+E5M2X4 = mybir.dt.float8_e5m2_x4
+ALU = mybir.AluOpType
+ACT = mybir.ActivationFunctionType
+
+P = 128
+PACK = 4
+LINE = 4
+HALF = ENTRIES // 2
+SCALAR_FROM = 336
+WINDOWS = 3
+
+
+def by_lines(planes):
+    return planes.rearrange("p t (c i) -> p c t i", i=LINE)
+
+
+def woven_by_lines(woven):
+    return woven.rearrange("p (c i) t -> p c t i", i=LINE)
+
+
+def flat(woven):
+    return woven.rearrange("p n t -> p (n t)")
+
+
+def tile_attend_gmhm_sm_kernel(tc, xT, mT, us, wt, te, y, offs, out):
+    nc = tc.nc
+    with ExitStack() as ctx:
+        keep = ctx.enter_context(tc.tile_pool(name="keep", bufs=1))
+        psum = ctx.enter_context(tc.psum_pool(name="psum", bufs=1))
+
+        offsets = keep.tile([P, ENTRIES // 16], U16, name="offsets")
+        x_raw = keep.tile([P, PACK, R], F32, name="x_raw")
+        memory = [keep.tile([P, PLACES], F32, name="memory%d" % j) for j in range(PACK)]
+        us_sb = keep.tile([P, PACK], F32, name="us_sb")
+        wt_sb = keep.tile([P, PACK], F32, name="wt_sb")
+        te_sb = keep.tile([P, ENTRIES], F32, name="te_sb")
+        y_sb = keep.tile([P, PACK, ENTRIES], F32, name="y_sb")
+
+        m_planes = mT.rearrange("(p j) c -> p j c", j=PACK)
+        nc.sync.dma_start(out=x_raw[:], in_=xT.rearrange("(p j) r -> p j r", j=PACK))
+        nc.sync.dma_start(offsets[:], offs)
+        nc.scalar.dma_start(out=us_sb[:], in_=us.rearrange("(s t) o -> s (t o)", t=PACK))
+        nc.scalar.dma_start(out=wt_sb[:], in_=wt.rearrange("(s t) o -> s (t o)", t=PACK))
+        for j in range(PACK):
+            nc.sync.dma_start(out=memory[j][:], in_=m_planes[:, j, :])
+        nc.sync.dma_start(out=te_sb[:], in_=te)
+        nc.sync.dma_start(out=y_sb[:], in_=y.rearrange("(s t) i -> s t i", t=PACK))
+
+        windows = [keep.tile([P, PLACES], F32, name="window%d" % w) for w in range(WINDOWS)]
+        for window in windows:
+            nc.vector.memset(window[:], 0.0)
+        identity = keep.tile([P, P], F32, name="identity")
+        make_identity(nc, identity[:])
+
+        xd_in = keep.tile([P, R, PACK], BF16, name="xd_in", align_bytes=64)
+        xd_codes = keep.tile([P, R], U32, name="xd_codes", align_bytes=64)
+        xd_scales = keep.tile([P, R], U8, name="xd_scales", align_bytes=64)
+        nc.scalar.activation(
+            out=xd_in[:].rearrange("p (t s) j -> p t s j", t=PACK),
+            in_=x_raw[:].rearrange("p j (s t) -> p t s j", t=PACK),
+            func=ACT.Copy,
+        )
+        nc.vector.quantize_mx(out=xd_codes[:].bitcast(E4M3X4), scales=xd_scales[:], in_=flat(xd_in[:]))
+
+        x_pairs = keep.tile([P, PACK, 2, P, 2], BF16, name="x_pairs")
+        for j in range(PACK):
+            nc.scalar.activation(
+                out=x_pairs[:, j],
+                in_=x_raw[:, j, :].rearrange("p (s u e) -> p u s e", u=2, e=2),
+                func=ACT.Copy,
+            )
+        x_words = x_pairs[:].rearrange("p j u s e -> p (j u s e)").bitcast(F32)
+        xr_in = keep.tile([P, D, PACK], BF16, name="xr_in", align_bytes=64)
+        xr_words = flat(xr_in[:]).bitcast(F32)
+        for h in range(2):
+            turned = psum.tile([P, 2, 2, P], F32, name="turned%d" % h, tag="side%d" % h)
+            for jj in range(2):
+                for u in range(2):
+                    at = ((2 * h + jj) * 2 + u) * P
+                    nc.tensor.transpose(turned[:, jj, u, :], x_words[:, at : at + P], identity[:])
+            nc.scalar.copy(
+                out=xr_words[:, h * 4 * P : (h + 1) * 4 * P].rearrange("s (j p u) -> s j p u", j=2, u=2),
+                in_=turned[:].rearrange("s j u p -> s j p u"),
+            )
+        xr_codes = keep.tile([P, D], U32, name="xr_codes", align_bytes=64)
+        xr_scales = keep.tile([P, D], U8, name="xr_scales", align_bytes=64)
+        nc.vector.quantize_mx(out=xr_codes[:].bitcast(E4M3X4), scales=xr_scales[:], in_=flat(xr_in[:]))
+
+        row_factor = keep.tile([P, PACK], F32, name="row_factor")
+        nc.vector.tensor_tensor(out=row_factor[:], in0=wt_sb[:], in1=us_sb[:], op=ALU.mult)
+
+        picked = keep.tile([P, PACK, ENTRIES], F32, name="picked")
+        for j in range(PACK):
+            nc.vector.tensor_copy(out=picked[:, j, :], in_=memory[j][:].indirect(offsets[:]))
+        m_in = keep.tile([P, ENTRIES, PACK], BF16, name="m_in", align_bytes=64)
+        m_codes = keep.tile([P, ENTRIES], U32, name="m_codes", align_bytes=64)
+        m_scales = keep.tile([P, ENTRIES], U8, name="m_scales", align_bytes=64)
+        for lo, hi in ((0, HALF), (HALF, SCALAR_FROM)):
+            nc.vector.tensor_copy(out=woven_by_lines(m_in[:, lo:hi, :]), in_=by_lines(picked[:, :, lo:hi]))
+        nc.scalar.copy(
+            out=woven_by_lines(m_in[:, SCALAR_FROM:, :]), in_=by_lines(picked[:, :, SCALAR_FROM:])
+        )
+        for lo in (0, HALF):
+            cols = slice(lo, lo + HALF)
+            nc.vector.quantize_mx(
+                out=m_codes[:, cols].bitcast(E4M3X4), scales=m_scales[:, cols], in_=flat(m_in[:, cols, :])
+            )
+
+        factor = keep.tile([P, PACK, ENTRIES], F32, name="factor")
+        for t in range(PACK):
+            nc.scalar.activation(
+                out=factor[:, t, :], in_=te_sb[:], func=ACT.Copy, scale=row_factor[:, t : t + 1]
+            )
+
+        z = keep.tile([P, PACK, ENTRIES], F32, name="z")
+        e = keep.tile([P, PACK, ENTRIES], F32, name="e")
+        diff = keep.tile([P, PACK, ENTRIES], F32, name="diff")
+        neg_max = keep.tile([P, PACK], F32, name="neg_max")
+        total = keep.tile([P, PACK], F32, name="total")
+        inverse = keep.tile([P, PACK], F32, name="inverse")
+
+        def logits(t):
+            rows = slice(t * P, (t + 1) * P)
+            scores = psum.tile([P, ENTRIES], F32, name="scores%d" % t)
+            nc.tensor.matmul_mx(
+                out=scores[:],
+                lhsT=xd_codes[:, rows].bitcast(E4M3X4),
+                lhsT_scale=xd_scales[:, rows],
+                rhs=m_codes[:].bitcast(E4M3X4),
+                rhs_scale=m_scales[:],
+                start=True,
+                stop=True,
+            )
+            nc.vector.scalar_tensor_tensor(
+                out=z[:, t, :],
+                in0=scores[:],
+                scalar=us_sb[:, t : t + 1],
+                in1=te_sb[:],
+                op0=ALU.mult,
+                op1=ALU.mult,
+            )
+
+        def exponentials(t):
+            one = slice(t, t + 1)
+            nc.vector.tensor_reduce(
+                out=neg_max[:, one], in_=z[:, t, :], axis=mybir.AxisListType.X, op=ALU.max, negate=True
+            )
+            nc.scalar.activation(
+                out=e[:, t, :], in_=z[:, t, :], func=ACT.Exp, bias=neg_max[:, one], accum_out=total[:, one]
+            )
+
+        def differences(t, cols):
+            nc.vector.scalar_tensor_tensor(
+                out=diff[:, t, cols],
+                in0=e[:, t, cols],
+                scalar=inverse[:, t : t + 1],
+                in1=y_sb[:, t, cols],
+                op0=ALU.mult,
+                op1=ALU.subtract,
+            )
+
+        logits(0)
+        for t in range(1, PACK):
+            logits(t)
+            exponentials(t - 1)
+        exponentials(PACK - 1)
+        nc.vector.reciprocal(out=inverse[:, 0:2], in_=total[:, 0:2])
+        differences(0, slice(0, ENTRIES))
+        nc.vector.reciprocal(out=inverse[:, 2:3], in_=total[:, 2:3])
+        differences(1, slice(0, ENTRIES))
+        nc.vector.reciprocal(out=inverse[:, 3:4], in_=total[:, 3:4])
+        differences(2, slice(0, ENTRIES))
+        differences(3, slice(0, HALF))
+        differences(3, slice(HALF, ENTRIES))
+
+        g_in = keep.tile([P, ENTRIES, PACK], BF16, name="g_in", align_bytes=64)
+        g_codes = keep.tile([P, ENTRIES], U32, name="g_codes", align_bytes=64)
+        g_scales = keep.tile([P, ENTRIES], U8, name="g_scales", align_bytes=64)
+        for lo in (0, HALF):
+            cols = slice(lo, lo + HALF)
+            nc.vector.tensor_tensor(
+                out=woven_by_lines(g_in[:, cols, :]),
+                in0=by_lines(diff[:, :, cols]),
+                in1=by_lines(factor[:, :, cols]),
+                op=ALU.mult,
+            )
+        for lo in (0, HALF):
+            cols = slice(lo, lo + HALF)
+            nc.vector.quantize_mx(
+                out=g_codes[:, cols].bitcast(E5M2X4), scales=g_scales[:, cols], in_=flat(g_in[:, cols, :])
+            )
+
+        out_planes = out.rearrange("(p j) c -> p j c", j=PACK)
+        for j in range(PACK):
+            feats = slice(j * P, (j + 1) * P)
+            sums = psum.tile([P, ENTRIES], F32, name="sums%d" % j, tag="side%d" % ((j + 2) % PACK))
+            nc.tensor.matmul_mx(
+                out=sums[:],
+                lhsT=xr_codes[:, feats].bitcast(E4M3X4),
+                lhsT_scale=xr_scales[:, feats],
+                rhs=g_codes[:].bitcast(E5M2X4),
+                rhs_scale=g_scales[:],
+                start=True,
+                stop=True,
+            )
+            dw = keep.tile([P, ENTRIES], F32, name="dw%d" % j)
+            nc.scalar.copy(out=dw[:], in_=sums[:])
+            window = windows[j % WINDOWS]
+            nc.vector.tensor_copy(out=window[:].indirect(offsets[:]), in_=dw[:])
+            nc.sync.dma_start(out=out_planes[:, j, :], in_=window[:])

@@ -22,6 +22,7 @@ LINE = 4
 HALF = ENTRIES // 2
 SCALAR_FROM = 336
 WINDOWS = 3
+X_SPLIT = 96
 
 
 def by_lines(planes):
@@ -40,6 +41,7 @@ def tile_attend_gmhm_sm_kernel(tc, xT, mT, us, wt, te, y, offs, out):
     nc = tc.nc
     with ExitStack() as ctx:
         keep = ctx.enter_context(tc.tile_pool(name="keep", bufs=1))
+        shared = ctx.enter_context(tc.tile_pool(name="shared", bufs=1))
         psum = ctx.enter_context(tc.psum_pool(name="psum", bufs=1))
 
         offsets = keep.tile([P, ENTRIES // 16], U16, name="offsets")
@@ -51,54 +53,21 @@ def tile_attend_gmhm_sm_kernel(tc, xT, mT, us, wt, te, y, offs, out):
         y_sb = keep.tile([P, PACK, ENTRIES], F32, name="y_sb")
 
         m_planes = mT.rearrange("(p j) c -> p j c", j=PACK)
-        nc.sync.dma_start(out=x_raw[:], in_=xT.rearrange("(p j) r -> p j r", j=PACK))
+        nc.sync.dma_start(out=memory[0][:], in_=m_planes[:, 0, :])
         nc.sync.dma_start(offsets[:], offs)
-        nc.scalar.dma_start(out=us_sb[:], in_=us.rearrange("(s t) o -> s (t o)", t=PACK))
-        nc.scalar.dma_start(out=wt_sb[:], in_=wt.rearrange("(s t) o -> s (t o)", t=PACK))
-        for j in range(PACK):
+        for j in range(1, PACK):
             nc.sync.dma_start(out=memory[j][:], in_=m_planes[:, j, :])
+        nc.sync.dma_start(out=x_raw[:], in_=xT.rearrange("(p j) r -> p j r", j=PACK))
         nc.sync.dma_start(out=te_sb[:], in_=te)
+        nc.sync.dma_start(out=us_sb[:], in_=us.rearrange("(s t) o -> s (t o)", t=PACK))
+        nc.sync.dma_start(out=wt_sb[:], in_=wt.rearrange("(s t) o -> s (t o)", t=PACK))
         nc.sync.dma_start(out=y_sb[:], in_=y.rearrange("(s t) i -> s t i", t=PACK))
 
         windows = [keep.tile([P, PLACES], F32, name="window%d" % w) for w in range(WINDOWS)]
         for window in windows:
             nc.vector.memset(window[:], 0.0)
-        identity = keep.tile([P, P], F32, name="identity")
+        identity = keep.tile([P, P], BF16, name="identity")
         make_identity(nc, identity[:])
-
-        xd_in = keep.tile([P, R, PACK], BF16, name="xd_in", align_bytes=64)
-        xd_codes = keep.tile([P, R], U32, name="xd_codes", align_bytes=64)
-        xd_scales = keep.tile([P, R], U8, name="xd_scales", align_bytes=64)
-        nc.scalar.activation(
-            out=xd_in[:].rearrange("p (t s) j -> p t s j", t=PACK),
-            in_=x_raw[:].rearrange("p j (s t) -> p t s j", t=PACK),
-            func=ACT.Copy,
-        )
-        nc.vector.quantize_mx(out=xd_codes[:].bitcast(E4M3X4), scales=xd_scales[:], in_=flat(xd_in[:]))
-
-        x_pairs = keep.tile([P, PACK, 2, P, 2], BF16, name="x_pairs")
-        for j in range(PACK):
-            nc.scalar.activation(
-                out=x_pairs[:, j],
-                in_=x_raw[:, j, :].rearrange("p (s u e) -> p u s e", u=2, e=2),
-                func=ACT.Copy,
-            )
-        x_words = x_pairs[:].rearrange("p j u s e -> p (j u s e)").bitcast(F32)
-        xr_in = keep.tile([P, D, PACK], BF16, name="xr_in", align_bytes=64)
-        xr_words = flat(xr_in[:]).bitcast(F32)
-        for h in range(2):
-            turned = psum.tile([P, 2, 2, P], F32, name="turned%d" % h, tag="side%d" % h)
-            for jj in range(2):
-                for u in range(2):
-                    at = ((2 * h + jj) * 2 + u) * P
-                    nc.tensor.transpose(turned[:, jj, u, :], x_words[:, at : at + P], identity[:])
-            nc.scalar.copy(
-                out=xr_words[:, h * 4 * P : (h + 1) * 4 * P].rearrange("s (j p u) -> s j p u", j=2, u=2),
-                in_=turned[:].rearrange("s j u p -> s j p u"),
-            )
-        xr_codes = keep.tile([P, D], U32, name="xr_codes", align_bytes=64)
-        xr_scales = keep.tile([P, D], U8, name="xr_scales", align_bytes=64)
-        nc.vector.quantize_mx(out=xr_codes[:].bitcast(E4M3X4), scales=xr_scales[:], in_=flat(xr_in[:]))
 
         row_factor = keep.tile([P, PACK], F32, name="row_factor")
         nc.vector.tensor_tensor(out=row_factor[:], in0=wt_sb[:], in1=us_sb[:], op=ALU.mult)
@@ -120,6 +89,19 @@ def tile_attend_gmhm_sm_kernel(tc, xT, mT, us, wt, te, y, offs, out):
                 out=m_codes[:, cols].bitcast(E4M3X4), scales=m_scales[:, cols], in_=flat(m_in[:, cols, :])
             )
 
+        xd_in = keep.tile([P, R, PACK], BF16, name="xd_in", align_bytes=64)
+        xd_codes = keep.tile([P, R], U32, name="xd_codes", align_bytes=64)
+        xd_scales = keep.tile([P, R], U8, name="xd_scales", align_bytes=64)
+        dealt = xd_in[:].rearrange("p (t s) j -> p s j t", t=PACK)
+        source = x_raw[:].rearrange("p j (s t) -> p s j t", t=PACK)
+        nc.scalar.activation(out=dealt[:, :X_SPLIT, :, :2], in_=source[:, :X_SPLIT, :, :2], func=ACT.Copy)
+        nc.vector.tensor_copy(out=dealt[:, X_SPLIT:, :, :2], in_=source[:, X_SPLIT:, :, :2])
+        nc.scalar.activation(out=dealt[:, :, :, 2:], in_=source[:, :, :, 2:], func=ACT.Copy)
+        for lo, hi in ((0, P), (P, 2 * P), (2 * P, R)):
+            nc.vector.quantize_mx(
+                out=xd_codes[:, lo:hi].bitcast(E4M3X4), scales=xd_scales[:, lo:hi], in_=flat(xd_in[:, lo:hi, :])
+            )
+
         factor = keep.tile([P, PACK, ENTRIES], F32, name="factor")
         for t in range(PACK):
             nc.scalar.activation(
@@ -127,7 +109,7 @@ def tile_attend_gmhm_sm_kernel(tc, xT, mT, us, wt, te, y, offs, out):
             )
 
         z = keep.tile([P, PACK, ENTRIES], F32, name="z")
-        e = keep.tile([P, PACK, ENTRIES], F32, name="e")
+        e = [keep.tile([P, ENTRIES], F32, name="e%d" % t, tag="e%d" % t, align_bytes=64) for t in range(PACK)]
         diff = keep.tile([P, PACK, ENTRIES], F32, name="diff")
         neg_max = keep.tile([P, PACK], F32, name="neg_max")
         total = keep.tile([P, PACK], F32, name="total")
@@ -135,7 +117,7 @@ def tile_attend_gmhm_sm_kernel(tc, xT, mT, us, wt, te, y, offs, out):
 
         def logits(t):
             rows = slice(t * P, (t + 1) * P)
-            scores = psum.tile([P, ENTRIES], F32, name="scores%d" % t)
+            scores = psum.tile([P, ENTRIES], F32, name="scores%d" % t, tag="first%d" % t)
             nc.tensor.matmul_mx(
                 out=scores[:],
                 lhsT=xd_codes[:, rows].bitcast(E4M3X4),
@@ -160,13 +142,13 @@ def tile_attend_gmhm_sm_kernel(tc, xT, mT, us, wt, te, y, offs, out):
                 out=neg_max[:, one], in_=z[:, t, :], axis=mybir.AxisListType.X, op=ALU.max, negate=True
             )
             nc.scalar.activation(
-                out=e[:, t, :], in_=z[:, t, :], func=ACT.Exp, bias=neg_max[:, one], accum_out=total[:, one]
+                out=e[t][:], in_=z[:, t, :], func=ACT.Exp, bias=neg_max[:, one], accum_out=total[:, one]
             )
 
         def differences(t, cols):
             nc.vector.scalar_tensor_tensor(
                 out=diff[:, t, cols],
-                in0=e[:, t, cols],
+                in0=e[t][:, cols],
                 scalar=inverse[:, t : t + 1],
                 in1=y_sb[:, t, cols],
                 op0=ALU.mult,
@@ -178,6 +160,12 @@ def tile_attend_gmhm_sm_kernel(tc, xT, mT, us, wt, te, y, offs, out):
             logits(t)
             exponentials(t - 1)
         exponentials(PACK - 1)
+        xr_in = keep.tile([P, D, PACK], BF16, name="xr_in", align_bytes=64)
+        for j in range(PACK):
+            turned = psum.tile([P, PACK, P], BF16, name="turned%d" % j, tag="first%d" % (2 + j % 2))
+            for t in range(PACK):
+                nc.tensor.transpose(turned[:, t, :], xd_in[:, t * P : (t + 1) * P, j], identity[:])
+            nc.scalar.copy(out=xr_in[:, j * P : (j + 1) * P, :], in_=turned[:].rearrange("s t p -> s p t"))
         nc.vector.reciprocal(out=inverse[:, 0:2], in_=total[:, 0:2])
         differences(0, slice(0, ENTRIES))
         nc.vector.reciprocal(out=inverse[:, 2:3], in_=total[:, 2:3])
@@ -187,38 +175,73 @@ def tile_attend_gmhm_sm_kernel(tc, xT, mT, us, wt, te, y, offs, out):
         differences(3, slice(0, HALF))
         differences(3, slice(HALF, ENTRIES))
 
-        g_in = keep.tile([P, ENTRIES, PACK], BF16, name="g_in", align_bytes=64)
-        g_codes = keep.tile([P, ENTRIES], U32, name="g_codes", align_bytes=64)
-        g_scales = keep.tile([P, ENTRIES], U8, name="g_scales", align_bytes=64)
-        for lo in (0, HALF):
-            cols = slice(lo, lo + HALF)
-            nc.vector.tensor_tensor(
-                out=woven_by_lines(g_in[:, cols, :]),
-                in0=by_lines(diff[:, :, cols]),
-                in1=by_lines(factor[:, :, cols]),
-                op=ALU.mult,
-            )
-        for lo in (0, HALF):
-            cols = slice(lo, lo + HALF)
+        xr_first = keep.tile([P, P], U32, name="xr_first", tag="e3", align_bytes=64)
+        xr_scales = keep.tile([P, D], U8, name="xr_scales", align_bytes=64)
+        g_in_a = shared.tile([P, HALF, PACK], BF16, name="g_in_a", align_bytes=64, offset=512)
+        g_in_b = shared.tile([P, HALF, PACK], BF16, name="g_in_b", align_bytes=64, offset=1536)
+        xr_rest = shared.tile([P, D - P], U32, name="xr_rest", align_bytes=64, offset=0)
+        xr_codes = [xr_first[:]] + [xr_rest[:, j * P : (j + 1) * P] for j in range(PACK - 1)]
+        g_codes = keep.tile([P, HALF + ENTRIES], U32, name="g_codes", align_bytes=64)
+        g_scales = keep.tile([P, HALF + ENTRIES], U8, name="g_scales", align_bytes=64)
+        nc.vector.memset(g_codes[:, :HALF], 0)
+        nc.vector.memset(g_scales[:, :HALF], 0)
+
+        def quantise_x(codes, lo, hi):
             nc.vector.quantize_mx(
-                out=g_codes[:, cols].bitcast(E5M2X4), scales=g_scales[:, cols], in_=flat(g_in[:, cols, :])
+                out=codes.bitcast(E4M3X4), scales=xr_scales[:, lo:hi], in_=flat(xr_in[:, lo:hi, :])
             )
 
-        out_planes = out.rearrange("(p j) c -> p j c", j=PACK)
-        for j in range(PACK):
+        def gradient(staged, lo, hi):
+            nc.vector.tensor_tensor(
+                out=woven_by_lines(staged[:]),
+                in0=by_lines(diff[:, :, lo:hi]),
+                in1=by_lines(factor[:, :, lo:hi]),
+                op=ALU.mult,
+            )
+
+        def quantise_g(staged, lo, hi):
+            cols = slice(HALF + lo, HALF + hi)
+            nc.vector.quantize_mx(
+                out=g_codes[:, cols].bitcast(E5M2X4), scales=g_scales[:, cols], in_=flat(staged[:])
+            )
+
+        def product(j, first, tag):
             feats = slice(j * P, (j + 1) * P)
-            sums = psum.tile([P, ENTRIES], F32, name="sums%d" % j, tag="side%d" % ((j + 2) % PACK))
+            cols = slice(first, first + ENTRIES)
+            sums = psum.tile([P, ENTRIES], F32, name="sums_" + tag, tag=tag)
             nc.tensor.matmul_mx(
                 out=sums[:],
-                lhsT=xr_codes[:, feats].bitcast(E4M3X4),
+                lhsT=xr_codes[j].bitcast(E4M3X4),
                 lhsT_scale=xr_scales[:, feats],
-                rhs=g_codes[:].bitcast(E5M2X4),
-                rhs_scale=g_scales[:],
+                rhs=g_codes[:, cols].bitcast(E5M2X4),
+                rhs_scale=g_scales[:, cols],
                 start=True,
                 stop=True,
             )
-            dw = keep.tile([P, ENTRIES], F32, name="dw%d" % j)
-            nc.scalar.copy(out=dw[:], in_=sums[:])
-            window = windows[j % WINDOWS]
-            nc.vector.tensor_copy(out=window[:].indirect(offsets[:]), in_=dw[:])
-            nc.sync.dma_start(out=out_planes[:, j, :], in_=window[:])
+            return sums
+
+        dw = keep.tile([P, PACK, ENTRIES], F32, name="dw")
+        out_planes = out.rearrange("(p j) c -> p j c", j=PACK)
+        window_of = [windows[0], windows[1], windows[2], windows[1]]
+
+        def scatter(j, lo, hi):
+            nc.vector.tensor_copy(
+                out=window_of[j][:].indirect(offsets[:, lo // 16 : hi // 16]), in_=dw[:, j, lo:hi]
+            )
+
+        gradient(g_in_a, 0, HALF)
+        quantise_x(xr_first[:], 0, P)
+        quantise_g(g_in_a, 0, HALF)
+        early = product(0, 0, "first0")
+        nc.scalar.copy(out=dw[:, 0, :HALF], in_=early[:, HALF:])
+        gradient(g_in_b, HALF, ENTRIES)
+        quantise_x(xr_rest[:, :P], P, 2 * P)
+        quantise_x(xr_rest[:, P:], 2 * P, D)
+        quantise_g(g_in_b, HALF, ENTRIES)
+        for j, lo in ((1, 0), (0, HALF), (2, 0), (3, 0)):
+            sums = product(j, HALF, "second%d" % j)
+            nc.scalar.copy(out=dw[:, j, lo:], in_=sums[:, lo:])
+        scatter(0, 0, HALF)
+        for j, lo in ((1, 0), (0, HALF), (2, 0), (3, 0)):
+            scatter(j, lo, ENTRIES)
+            nc.sync.dma_start(out=out_planes[:, j, :], in_=window_of[j][:])

@@ -22,7 +22,7 @@ LINE = 4
 HALF = ENTRIES // 2
 SCALAR_FROM = 336
 WINDOWS = 3
-X_SPLIT = 96
+X_SPLIT = 64
 
 
 def by_lines(planes):
@@ -45,7 +45,7 @@ def tile_attend_gmhm_sm_kernel(tc, xT, mT, us, wt, te, y, offs, out):
         psum = ctx.enter_context(tc.psum_pool(name="psum", bufs=1))
 
         offsets = keep.tile([P, ENTRIES // 16], U16, name="offsets")
-        x_raw = keep.tile([P, PACK, R], F32, name="x_raw")
+        x_raw = keep.tile([P, PACK, R], F32, name="x_raw", tag="x_raw")
         memory = [keep.tile([P, PLACES], F32, name="memory%d" % j) for j in range(PACK)]
         us_sb = keep.tile([P, PACK], F32, name="us_sb")
         wt_sb = keep.tile([P, PACK], F32, name="wt_sb")
@@ -102,15 +102,12 @@ def tile_attend_gmhm_sm_kernel(tc, xT, mT, us, wt, te, y, offs, out):
                 out=xd_codes[:, lo:hi].bitcast(E4M3X4), scales=xd_scales[:, lo:hi], in_=flat(xd_in[:, lo:hi, :])
             )
 
-        factor = keep.tile([P, PACK, ENTRIES], F32, name="factor")
-        for t in range(PACK):
-            nc.scalar.activation(
-                out=factor[:, t, :], in_=te_sb[:], func=ACT.Copy, scale=row_factor[:, t : t + 1]
-            )
-
-        z = keep.tile([P, PACK, ENTRIES], F32, name="z")
+        z = keep.tile([P, PACK, ENTRIES], F32, name="z", tag="x_raw")
         e = [keep.tile([P, ENTRIES], F32, name="e%d" % t, tag="e%d" % t, align_bytes=64) for t in range(PACK)]
         diff = keep.tile([P, PACK, ENTRIES], F32, name="diff")
+        factor_row = keep.tile([P, PACK * ENTRIES], F32, name="factor_row")
+        factor = factor_row[:].rearrange("p (t i) -> p t i", t=PACK)
+        scaled = factor[:, 3, :]
         neg_max = keep.tile([P, PACK], F32, name="neg_max")
         total = keep.tile([P, PACK], F32, name="total")
         inverse = keep.tile([P, PACK], F32, name="inverse")
@@ -127,6 +124,10 @@ def tile_attend_gmhm_sm_kernel(tc, xT, mT, us, wt, te, y, offs, out):
                 start=True,
                 stop=True,
             )
+            if t == 2:
+                nc.scalar.activation(out=scaled, in_=scores[:], func=ACT.Copy, scale=us_sb[:, t : t + 1])
+                nc.gpsimd.tensor_tensor(out=z[:, t, :], in0=scaled, in1=te_sb[:], op=ALU.mult)
+                return
             nc.vector.scalar_tensor_tensor(
                 out=z[:, t, :],
                 in0=scores[:],
@@ -156,10 +157,26 @@ def tile_attend_gmhm_sm_kernel(tc, xT, mT, us, wt, te, y, offs, out):
             )
 
         logits(0)
-        for t in range(1, PACK):
-            logits(t)
-            exponentials(t - 1)
-        exponentials(PACK - 1)
+        logits(1)
+        exponentials(0)
+        logits(2)
+        logits(3)
+        for t in (1, 3, 2):
+            exponentials(t)
+        for t in range(3):
+            nc.scalar.activation(
+                out=factor[:, t, :], in_=te_sb[:], func=ACT.Copy, scale=row_factor[:, t : t + 1]
+            )
+        for t in range(3, PACK):
+            nc.gpsimd.tensor_scalar(
+                out=factor[:, t, :],
+                in0=te_sb[:],
+                scalar1=row_factor[:, t : t + 1],
+                scalar2=0.0,
+                op0=ALU.mult,
+                op1=ALU.add,
+            )
+
         xr_in = keep.tile([P, D, PACK], BF16, name="xr_in", align_bytes=64)
         for j in range(PACK):
             turned = psum.tile([P, PACK, P], BF16, name="turned%d" % j, tag="first%d" % (2 + j % 2))
@@ -168,14 +185,14 @@ def tile_attend_gmhm_sm_kernel(tc, xT, mT, us, wt, te, y, offs, out):
             nc.scalar.copy(out=xr_in[:, j * P : (j + 1) * P, :], in_=turned[:].rearrange("s t p -> s p t"))
         nc.vector.reciprocal(out=inverse[:, 0:2], in_=total[:, 0:2])
         differences(0, slice(0, ENTRIES))
-        nc.vector.reciprocal(out=inverse[:, 2:3], in_=total[:, 2:3])
-        differences(1, slice(0, ENTRIES))
         nc.vector.reciprocal(out=inverse[:, 3:4], in_=total[:, 3:4])
-        differences(2, slice(0, ENTRIES))
-        differences(3, slice(0, HALF))
-        differences(3, slice(HALF, ENTRIES))
+        differences(1, slice(0, ENTRIES))
+        nc.vector.reciprocal(out=inverse[:, 2:3], in_=total[:, 2:3])
+        differences(3, slice(0, ENTRIES))
+        differences(2, slice(0, HALF))
+        differences(2, slice(HALF, ENTRIES))
 
-        xr_first = keep.tile([P, P], U32, name="xr_first", tag="e3", align_bytes=64)
+        xr_first = keep.tile([P, P], U32, name="xr_first", tag="e2", align_bytes=64)
         xr_scales = keep.tile([P, D], U8, name="xr_scales", align_bytes=64)
         g_in_a = shared.tile([P, HALF, PACK], BF16, name="g_in_a", align_bytes=64, offset=512)
         g_in_b = shared.tile([P, HALF, PACK], BF16, name="g_in_b", align_bytes=64, offset=1536)

@@ -18,19 +18,23 @@ ACT = mybir.ActivationFunctionType
 
 P = 128
 PACK = 4
-LINE = 4
+RUN = 4
 HALF = ENTRIES // 2
-SCALAR_FROM = 336
+LIST_ROWS = 16
 WINDOWS = 3
-X_SPLIT = 64
+SCALAR_FROM = 336
+ASIDE = 2
+EARLY = 2
+
+X_LATE_AT, G_FIRST_AT, G_SECOND_AT = 0, 512, 1536
 
 
-def by_lines(planes):
-    return planes.rearrange("p t (c i) -> p c t i", i=LINE)
+def in_runs(planes):
+    return planes.rearrange("p t (c i) -> p c t i", i=RUN)
 
 
-def woven_by_lines(woven):
-    return woven.rearrange("p (c i) t -> p c t i", i=LINE)
+def woven_in_runs(woven):
+    return woven.rearrange("p (c i) t -> p c t i", i=RUN)
 
 
 def flat(woven):
@@ -44,7 +48,7 @@ def tile_attend_gmhm_sm_kernel(tc, xT, mT, us, wt, te, y, offs, out):
         shared = ctx.enter_context(tc.tile_pool(name="shared", bufs=1))
         psum = ctx.enter_context(tc.psum_pool(name="psum", bufs=1))
 
-        offsets = keep.tile([P, ENTRIES // 16], U16, name="offsets")
+        offsets = keep.tile([P, ENTRIES // LIST_ROWS], U16, name="offsets")
         x_raw = keep.tile([P, PACK, R], F32, name="x_raw", tag="x_raw")
         memory = [keep.tile([P, PLACES], F32, name="memory%d" % j) for j in range(PACK)]
         us_sb = keep.tile([P, PACK], F32, name="us_sb")
@@ -66,7 +70,7 @@ def tile_attend_gmhm_sm_kernel(tc, xT, mT, us, wt, te, y, offs, out):
         windows = [keep.tile([P, PLACES], F32, name="window%d" % w) for w in range(WINDOWS)]
         for window in windows:
             nc.vector.memset(window[:], 0.0)
-        identity = keep.tile([P, P], BF16, name="identity")
+        identity = keep.tile([P, P], F32, name="identity")
         make_identity(nc, identity[:])
 
         row_factor = keep.tile([P, PACK], F32, name="row_factor")
@@ -79,10 +83,8 @@ def tile_attend_gmhm_sm_kernel(tc, xT, mT, us, wt, te, y, offs, out):
         m_codes = keep.tile([P, ENTRIES], U32, name="m_codes", align_bytes=64)
         m_scales = keep.tile([P, ENTRIES], U8, name="m_scales", align_bytes=64)
         for lo, hi in ((0, HALF), (HALF, SCALAR_FROM)):
-            nc.vector.tensor_copy(out=woven_by_lines(m_in[:, lo:hi, :]), in_=by_lines(picked[:, :, lo:hi]))
-        nc.scalar.copy(
-            out=woven_by_lines(m_in[:, SCALAR_FROM:, :]), in_=by_lines(picked[:, :, SCALAR_FROM:])
-        )
+            nc.vector.tensor_copy(out=woven_in_runs(m_in[:, lo:hi, :]), in_=in_runs(picked[:, :, lo:hi]))
+        nc.scalar.copy(out=woven_in_runs(m_in[:, SCALAR_FROM:, :]), in_=in_runs(picked[:, :, SCALAR_FROM:]))
         for lo in (0, HALF):
             cols = slice(lo, lo + HALF)
             nc.vector.quantize_mx(
@@ -94,8 +96,8 @@ def tile_attend_gmhm_sm_kernel(tc, xT, mT, us, wt, te, y, offs, out):
         xd_scales = keep.tile([P, R], U8, name="xd_scales", align_bytes=64)
         dealt = xd_in[:].rearrange("p (t s) j -> p s j t", t=PACK)
         source = x_raw[:].rearrange("p j (s t) -> p s j t", t=PACK)
-        nc.scalar.activation(out=dealt[:, :X_SPLIT, :, :2], in_=source[:, :X_SPLIT, :, :2], func=ACT.Copy)
-        nc.vector.tensor_copy(out=dealt[:, X_SPLIT:, :, :2], in_=source[:, X_SPLIT:, :, :2])
+        nc.scalar.activation(out=dealt[:, : P // 2, :, :2], in_=source[:, : P // 2, :, :2], func=ACT.Copy)
+        nc.vector.tensor_copy(out=dealt[:, P // 2 :, :, :2], in_=source[:, P // 2 :, :, :2])
         nc.scalar.activation(out=dealt[:, :, :, 2:], in_=source[:, :, :, 2:], func=ACT.Copy)
         for lo, hi in ((0, P), (P, 2 * P), (2 * P, R)):
             nc.vector.quantize_mx(
@@ -105,14 +107,13 @@ def tile_attend_gmhm_sm_kernel(tc, xT, mT, us, wt, te, y, offs, out):
         z = keep.tile([P, PACK, ENTRIES], F32, name="z", tag="x_raw")
         e = [keep.tile([P, ENTRIES], F32, name="e%d" % t, tag="e%d" % t, align_bytes=64) for t in range(PACK)]
         diff = keep.tile([P, PACK, ENTRIES], F32, name="diff")
-        factor_row = keep.tile([P, PACK * ENTRIES], F32, name="factor_row")
-        factor = factor_row[:].rearrange("p (t i) -> p t i", t=PACK)
-        scaled = factor[:, 3, :]
+        factor = keep.tile([P, PACK, ENTRIES], F32, name="factor")
         neg_max = keep.tile([P, PACK], F32, name="neg_max")
         total = keep.tile([P, PACK], F32, name="total")
         inverse = keep.tile([P, PACK], F32, name="inverse")
+        last = PACK - 1
 
-        def logits(t):
+        def scores_of(t):
             rows = slice(t * P, (t + 1) * P)
             scores = psum.tile([P, ENTRIES], F32, name="scores%d" % t, tag="first%d" % t)
             nc.tensor.matmul_mx(
@@ -124,18 +125,22 @@ def tile_attend_gmhm_sm_kernel(tc, xT, mT, us, wt, te, y, offs, out):
                 start=True,
                 stop=True,
             )
-            if t == 2:
-                nc.scalar.activation(out=scaled, in_=scores[:], func=ACT.Copy, scale=us_sb[:, t : t + 1])
-                nc.gpsimd.tensor_tensor(out=z[:, t, :], in0=scaled, in1=te_sb[:], op=ALU.mult)
-                return
+            return scores
+
+        def logits(t):
             nc.vector.scalar_tensor_tensor(
                 out=z[:, t, :],
-                in0=scores[:],
+                in0=scores_of(t)[:],
                 scalar=us_sb[:, t : t + 1],
                 in1=te_sb[:],
                 op0=ALU.mult,
                 op1=ALU.mult,
             )
+
+        def logits_aside(t):
+            scaled = factor[:, last, :]
+            nc.scalar.activation(out=scaled, in_=scores_of(t)[:], func=ACT.Copy, scale=us_sb[:, t : t + 1])
+            nc.gpsimd.tensor_tensor(out=z[:, t, :], in0=scaled, in1=te_sb[:], op=ALU.mult)
 
         def exponentials(t):
             one = slice(t, t + 1)
@@ -145,6 +150,9 @@ def tile_attend_gmhm_sm_kernel(tc, xT, mT, us, wt, te, y, offs, out):
             nc.scalar.activation(
                 out=e[t][:], in_=z[:, t, :], func=ACT.Exp, bias=neg_max[:, one], accum_out=total[:, one]
             )
+
+        def invert(lo, hi):
+            nc.vector.reciprocal(out=inverse[:, lo:hi], in_=total[:, lo:hi])
 
         def differences(t, cols):
             nc.vector.scalar_tensor_tensor(
@@ -159,45 +167,50 @@ def tile_attend_gmhm_sm_kernel(tc, xT, mT, us, wt, te, y, offs, out):
         logits(0)
         logits(1)
         exponentials(0)
-        logits(2)
-        logits(3)
-        for t in (1, 3, 2):
+        logits_aside(ASIDE)
+        logits(last)
+        for t in (1, last, ASIDE):
             exponentials(t)
-        for t in range(3):
-            nc.scalar.activation(
-                out=factor[:, t, :], in_=te_sb[:], func=ACT.Copy, scale=row_factor[:, t : t + 1]
-            )
-        for t in range(3, PACK):
-            nc.gpsimd.tensor_scalar(
-                out=factor[:, t, :],
-                in0=te_sb[:],
-                scalar1=row_factor[:, t : t + 1],
-                scalar2=0.0,
-                op0=ALU.mult,
-                op1=ALU.add,
-            )
+
+        for t in range(last):
+            nc.scalar.activation(out=factor[:, t, :], in_=te_sb[:], func=ACT.Copy, scale=row_factor[:, t : t + 1])
+        nc.gpsimd.tensor_scalar(
+            out=factor[:, last, :],
+            in0=te_sb[:],
+            scalar1=row_factor[:, last:],
+            scalar2=0.0,
+            op0=ALU.mult,
+            op1=ALU.add,
+        )
 
         xr_in = keep.tile([P, D, PACK], BF16, name="xr_in", align_bytes=64)
-        for j in range(PACK):
-            turned = psum.tile([P, PACK, P], BF16, name="turned%d" % j, tag="first%d" % (2 + j % 2))
+        pairs = flat(xd_in[:]).bitcast(F32).rearrange("p (n h) -> p n h", h=2)
+        for h in range(2):
+            turned = psum.tile([P, PACK, P], F32, name="turned%d" % h, tag="first%d" % (2 + h))
             for t in range(PACK):
-                nc.tensor.transpose(turned[:, t, :], xd_in[:, t * P : (t + 1) * P, j], identity[:])
-            nc.scalar.copy(out=xr_in[:, j * P : (j + 1) * P, :], in_=turned[:].rearrange("s t p -> s p t"))
-        nc.vector.reciprocal(out=inverse[:, 0:2], in_=total[:, 0:2])
-        differences(0, slice(0, ENTRIES))
-        nc.vector.reciprocal(out=inverse[:, 3:4], in_=total[:, 3:4])
-        differences(1, slice(0, ENTRIES))
-        nc.vector.reciprocal(out=inverse[:, 2:3], in_=total[:, 2:3])
-        differences(3, slice(0, ENTRIES))
-        differences(2, slice(0, HALF))
-        differences(2, slice(HALF, ENTRIES))
+                nc.tensor.transpose(turned[:, t, :], pairs[:, t * P : (t + 1) * P, h], identity[:])
+            parted = turned[:].rearrange("s t p -> s (t p)").bitcast(BF16)
+            parted = parted.rearrange("s (t p m) -> s m p t", t=PACK, m=2)
+            for member in range(2):
+                j = 2 * h + member
+                nc.scalar.copy(out=xr_in[:, j * P : (j + 1) * P, :], in_=parted[:, member])
 
-        xr_first = keep.tile([P, P], U32, name="xr_first", tag="e2", align_bytes=64)
+        invert(0, 2)
+        differences(0, slice(0, ENTRIES))
+        invert(last, PACK)
+        differences(1, slice(0, ENTRIES))
+        invert(ASIDE, ASIDE + 1)
+        differences(last, slice(0, ENTRIES))
+        differences(ASIDE, slice(0, HALF))
+        differences(ASIDE, slice(HALF, ENTRIES))
+
+        xr_early = keep.tile([P, EARLY * P], U32, name="xr_early", tag="e%d" % ASIDE, align_bytes=64)
         xr_scales = keep.tile([P, D], U8, name="xr_scales", align_bytes=64)
-        g_in_a = shared.tile([P, HALF, PACK], BF16, name="g_in_a", align_bytes=64, offset=512)
-        g_in_b = shared.tile([P, HALF, PACK], BF16, name="g_in_b", align_bytes=64, offset=1536)
-        xr_rest = shared.tile([P, D - P], U32, name="xr_rest", align_bytes=64, offset=0)
-        xr_codes = [xr_first[:]] + [xr_rest[:, j * P : (j + 1) * P] for j in range(PACK - 1)]
+        g_first = shared.tile([P, HALF, PACK], BF16, name="g_first", align_bytes=64, offset=G_FIRST_AT)
+        g_second = shared.tile([P, HALF, PACK], BF16, name="g_second", align_bytes=64, offset=G_SECOND_AT)
+        xr_late = shared.tile([P, D - EARLY * P], U32, name="xr_late", align_bytes=64, offset=X_LATE_AT)
+        xr_codes = [xr_early[:, j * P : (j + 1) * P] for j in range(EARLY)]
+        xr_codes.extend(xr_late[:, j * P : (j + 1) * P] for j in range(PACK - EARLY))
         g_codes = keep.tile([P, HALF + ENTRIES], U32, name="g_codes", align_bytes=64)
         g_scales = keep.tile([P, HALF + ENTRIES], U8, name="g_scales", align_bytes=64)
         nc.vector.memset(g_codes[:, :HALF], 0)
@@ -208,24 +221,24 @@ def tile_attend_gmhm_sm_kernel(tc, xT, mT, us, wt, te, y, offs, out):
                 out=codes.bitcast(E4M3X4), scales=xr_scales[:, lo:hi], in_=flat(xr_in[:, lo:hi, :])
             )
 
-        def gradient(staged, lo, hi):
+        def gradient(woven, lo, hi):
             nc.vector.tensor_tensor(
-                out=woven_by_lines(staged[:]),
-                in0=by_lines(diff[:, :, lo:hi]),
-                in1=by_lines(factor[:, :, lo:hi]),
+                out=woven_in_runs(woven[:]),
+                in0=in_runs(diff[:, :, lo:hi]),
+                in1=in_runs(factor[:, :, lo:hi]),
                 op=ALU.mult,
             )
 
-        def quantise_g(staged, lo, hi):
+        def quantise_g(woven, lo, hi):
             cols = slice(HALF + lo, HALF + hi)
             nc.vector.quantize_mx(
-                out=g_codes[:, cols].bitcast(E5M2X4), scales=g_scales[:, cols], in_=flat(staged[:])
+                out=g_codes[:, cols].bitcast(E5M2X4), scales=g_scales[:, cols], in_=flat(woven[:])
             )
 
-        def product(j, first, tag):
+        def product(j, first_column, bank):
             feats = slice(j * P, (j + 1) * P)
-            cols = slice(first, first + ENTRIES)
-            sums = psum.tile([P, ENTRIES], F32, name="sums_" + tag, tag=tag)
+            cols = slice(first_column, first_column + ENTRIES)
+            sums = psum.tile([P, ENTRIES], F32, name="sums_" + bank, tag=bank)
             nc.tensor.matmul_mx(
                 out=sums[:],
                 lhsT=xr_codes[j].bitcast(E4M3X4),
@@ -239,26 +252,26 @@ def tile_attend_gmhm_sm_kernel(tc, xT, mT, us, wt, te, y, offs, out):
 
         dw = keep.tile([P, PACK, ENTRIES], F32, name="dw")
         out_planes = out.rearrange("(p j) c -> p j c", j=PACK)
-        window_of = [windows[0], windows[1], windows[2], windows[1]]
 
         def scatter(j, lo, hi):
-            nc.vector.tensor_copy(
-                out=window_of[j][:].indirect(offsets[:, lo // 16 : hi // 16]), in_=dw[:, j, lo:hi]
-            )
+            listed = offsets[:, lo // LIST_ROWS : hi // LIST_ROWS]
+            nc.vector.tensor_copy(out=windows[j % WINDOWS][:].indirect(listed), in_=dw[:, j, lo:hi])
 
-        gradient(g_in_a, 0, HALF)
-        quantise_x(xr_first[:], 0, P)
-        quantise_g(g_in_a, 0, HALF)
-        early = product(0, 0, "first0")
-        nc.scalar.copy(out=dw[:, 0, :HALF], in_=early[:, HALF:])
-        gradient(g_in_b, HALF, ENTRIES)
-        quantise_x(xr_rest[:, :P], P, 2 * P)
-        quantise_x(xr_rest[:, P:], 2 * P, D)
-        quantise_g(g_in_b, HALF, ENTRIES)
-        for j, lo in ((1, 0), (0, HALF), (2, 0), (3, 0)):
+        gradient(g_first, 0, HALF)
+        quantise_x(xr_early[:], 0, EARLY * P)
+        quantise_g(g_first, 0, HALF)
+        for j in range(EARLY):
+            sums = product(j, 0, "first%d" % j)
+            nc.scalar.copy(out=dw[:, j, :HALF], in_=sums[:, HALF:])
+        gradient(g_second, HALF, ENTRIES)
+        quantise_x(xr_late[:], EARLY * P, D)
+        quantise_g(g_second, HALF, ENTRIES)
+        still_from = [HALF if j < EARLY else 0 for j in range(PACK)]
+        for j in range(PACK):
             sums = product(j, HALF, "second%d" % j)
-            nc.scalar.copy(out=dw[:, j, lo:], in_=sums[:, lo:])
-        scatter(0, 0, HALF)
-        for j, lo in ((1, 0), (0, HALF), (2, 0), (3, 0)):
-            scatter(j, lo, ENTRIES)
-            nc.sync.dma_start(out=out_planes[:, j, :], in_=window_of[j][:])
+            nc.scalar.copy(out=dw[:, j, still_from[j] :], in_=sums[:, still_from[j] :])
+        for j in range(EARLY):
+            scatter(j, 0, HALF)
+        for j in range(PACK):
+            scatter(j, still_from[j], ENTRIES)
+            nc.sync.dma_start(out=out_planes[:, j, :], in_=windows[j % WINDOWS][:])

@@ -49,7 +49,7 @@ def tile_attend_gmhm_sm_kernel(tc, xT, mT, us, wt, te, y, offs, out):
         psum = ctx.enter_context(tc.psum_pool(name="psum", bufs=1))
 
         offsets = keep.tile([P, ENTRIES // LIST_ROWS], U16, name="offsets")
-        x_raw = keep.tile([P, PACK, R], F32, name="x_raw", tag="x_raw")
+        x_raw = keep.tile([P, PACK, R], F32, name="x_raw", tag="x_raw", align_bytes=64)
         memory = [keep.tile([P, PLACES], F32, name="memory%d" % j) for j in range(PACK)]
         us_sb = keep.tile([P, PACK], F32, name="us_sb")
         wt_sb = keep.tile([P, PACK], F32, name="wt_sb")
@@ -104,7 +104,7 @@ def tile_attend_gmhm_sm_kernel(tc, xT, mT, us, wt, te, y, offs, out):
                 out=xd_codes[:, lo:hi].bitcast(E4M3X4), scales=xd_scales[:, lo:hi], in_=flat(xd_in[:, lo:hi, :])
             )
 
-        z = keep.tile([P, PACK, ENTRIES], F32, name="z", tag="x_raw")
+        z = keep.tile([P, PACK, ENTRIES], F32, name="z", tag="x_raw", align_bytes=64)
         e = [keep.tile([P, ENTRIES], F32, name="e%d" % t, tag="e%d" % t, align_bytes=64) for t in range(PACK)]
         diff = keep.tile([P, PACK, ENTRIES], F32, name="diff")
         factor = keep.tile([P, PACK, ENTRIES], F32, name="factor")
@@ -183,7 +183,7 @@ def tile_attend_gmhm_sm_kernel(tc, xT, mT, us, wt, te, y, offs, out):
             op1=ALU.add,
         )
 
-        xr_in = keep.tile([P, D, PACK], BF16, name="xr_in", align_bytes=64)
+        xr_in = keep.tile([P, D, PACK], BF16, name="xr_in", tag="x_raw", align_bytes=64)
         pairs = flat(xd_in[:]).bitcast(F32).rearrange("p (n h) -> p n h", h=2)
         for h in range(2):
             turned = psum.tile([P, PACK, P], F32, name="turned%d" % h, tag="first%d" % (2 + h))

@@ -200,11 +200,11 @@ def tile_attend_gmhm_sm_kernel(tc, xT, mT, us, wt, te, y, offs, out):
         invert(last, PACK)
         differences(1, slice(0, ENTRIES))
         invert(ASIDE, ASIDE + 1)
-        differences(last, slice(0, ENTRIES))
+        differences(last, slice(0, HALF))
         differences(ASIDE, slice(0, HALF))
-        differences(ASIDE, slice(HALF, ENTRIES))
+        differences(last, slice(HALF, ENTRIES))
 
-        xr_early = keep.tile([P, EARLY * P], U32, name="xr_early", tag="e%d" % ASIDE, align_bytes=64)
+        xr_early = keep.tile([P, EARLY * P], U32, name="xr_early", align_bytes=64)
         xr_scales = keep.tile([P, D], U8, name="xr_scales", align_bytes=64)
         g_first = shared.tile([P, HALF, PACK], BF16, name="g_first", align_bytes=64, offset=G_FIRST_AT)
         g_second = shared.tile([P, HALF, PACK], BF16, name="g_second", align_bytes=64, offset=G_SECOND_AT)
@@ -263,6 +263,7 @@ def tile_attend_gmhm_sm_kernel(tc, xT, mT, us, wt, te, y, offs, out):
         for j in range(EARLY):
             sums = product(j, 0, "first%d" % j)
             nc.scalar.copy(out=dw[:, j, :HALF], in_=sums[:, HALF:])
+        differences(ASIDE, slice(HALF, ENTRIES))
         gradient(g_second, HALF, ENTRIES)
         quantise_x(xr_late[:], EARLY * P, D)
         quantise_g(g_second, HALF, ENTRIES)

@@ -62,9 +62,9 @@ def tile_attend_gmhm_sm_kernel(tc, xT, mT, us, wt, te, y, offs, out):
         for j in range(1, PACK):
             nc.sync.dma_start(out=memory[j][:], in_=m_planes[:, j, :])
         nc.sync.dma_start(out=x_raw[:], in_=xT.rearrange("(p j) r -> p j r", j=PACK))
-        nc.sync.dma_start(out=te_sb[:], in_=te)
         nc.sync.dma_start(out=us_sb[:], in_=us.rearrange("(s t) o -> s (t o)", t=PACK))
         nc.sync.dma_start(out=wt_sb[:], in_=wt.rearrange("(s t) o -> s (t o)", t=PACK))
+        nc.sync.dma_start(out=te_sb[:], in_=te)
         nc.sync.dma_start(out=y_sb[:], in_=y.rearrange("(s t) i -> s t i", t=PACK))
 
         windows = [keep.tile([P, PLACES], F32, name="window%d" % w) for w in range(WINDOWS)]

@@ -21,12 +21,10 @@ PACK = 4
 RUN = 4
 HALF = ENTRIES // 2
 LIST_ROWS = 16
-WINDOWS = 3
-SCALAR_FROM = 336
 ASIDE = 2
-EARLY = 2
-
-X_LATE_AT, G_FIRST_AT, G_SECOND_AT = 0, 512, 1536
+SCALAR_FROM = 336
+QUARTERS = ENTRIES // P
+REST = ENTRIES - P
 
 
 def in_runs(planes):
@@ -48,15 +46,21 @@ def tile_attend_gmhm_sm_kernel(tc, xT, mT, us, wt, te, y, offs, out):
         shared = ctx.enter_context(tc.tile_pool(name="shared", bufs=1))
         psum = ctx.enter_context(tc.psum_pool(name="psum", bufs=1))
 
+        def bank(number, shape, name):
+            return psum.tile([P] + shape, F32, name=name, tag="bank%d" % number)
+
         offsets = keep.tile([P, ENTRIES // LIST_ROWS], U16, name="offsets")
         x_raw = keep.tile([P, PACK, R], F32, name="x_raw", tag="x_raw", align_bytes=64)
         memory = [keep.tile([P, PLACES], F32, name="memory%d" % j) for j in range(PACK)]
         us_sb = keep.tile([P, PACK], F32, name="us_sb")
         wt_sb = keep.tile([P, PACK], F32, name="wt_sb")
         te_sb = keep.tile([P, ENTRIES], F32, name="te_sb")
-        y_sb = keep.tile([P, PACK, ENTRIES], F32, name="y_sb")
+        y_first = keep.tile([P, PACK, P], F32, name="y_first")
+        y_low = keep.tile([P, 2, REST], F32, name="y_low")
+        y_high = keep.tile([P, 2, REST], F32, name="y_high")
 
         m_planes = mT.rearrange("(p j) c -> p j c", j=PACK)
+        y_tiles = y.rearrange("(s t) i -> s t i", t=PACK)
         nc.sync.dma_start(out=memory[0][:], in_=m_planes[:, 0, :])
         nc.sync.dma_start(offsets[:], offs)
         for j in range(1, PACK):
@@ -65,16 +69,19 @@ def tile_attend_gmhm_sm_kernel(tc, xT, mT, us, wt, te, y, offs, out):
         nc.sync.dma_start(out=us_sb[:], in_=us.rearrange("(s t) o -> s (t o)", t=PACK))
         nc.sync.dma_start(out=wt_sb[:], in_=wt.rearrange("(s t) o -> s (t o)", t=PACK))
         nc.sync.dma_start(out=te_sb[:], in_=te)
-        nc.sync.dma_start(out=y_sb[:], in_=y.rearrange("(s t) i -> s t i", t=PACK))
+        nc.sync.dma_start(out=y_first[:], in_=y_tiles[:, :, :P])
+        nc.sync.dma_start(out=y_low[:], in_=y_tiles[:, :2, P:])
+        nc.sync.dma_start(out=y_high[:], in_=y_tiles[:, 2:, P:])
 
-        windows = [keep.tile([P, PLACES], F32, name="window%d" % w) for w in range(WINDOWS)]
-        for window in windows:
-            nc.vector.memset(window[:], 0.0)
+        windows = [keep.tile([P, PLACES], F32, name="window%d" % w) for w in range(PACK)]
         identity = keep.tile([P, P], F32, name="identity")
         make_identity(nc, identity[:])
+        for window in windows[:-1]:
+            nc.vector.memset(window[:], 0.0)
+        nc.gpsimd.memset(windows[-1][:], 0.0)
 
         row_factor = keep.tile([P, PACK], F32, name="row_factor")
-        nc.vector.tensor_tensor(out=row_factor[:], in0=wt_sb[:], in1=us_sb[:], op=ALU.mult)
+        nc.gpsimd.tensor_tensor(out=row_factor[:], in0=wt_sb[:], in1=us_sb[:], op=ALU.mult)
 
         picked = keep.tile([P, PACK, ENTRIES], F32, name="picked")
         for j in range(PACK):
@@ -105,17 +112,23 @@ def tile_attend_gmhm_sm_kernel(tc, xT, mT, us, wt, te, y, offs, out):
             )
 
         z = keep.tile([P, PACK, ENTRIES], F32, name="z", tag="x_raw", align_bytes=64)
-        e = [keep.tile([P, ENTRIES], F32, name="e%d" % t, tag="e%d" % t, align_bytes=64) for t in range(PACK)]
-        diff = keep.tile([P, PACK, ENTRIES], F32, name="diff")
-        factor = keep.tile([P, PACK, ENTRIES], F32, name="factor")
+        e = [keep.tile([P, ENTRIES], F32, name="e%d" % t) for t in range(PACK)]
+        scaled = shared.tile([P, ENTRIES], F32, name="scaled", offset=0)
+        diff = keep.tile([P, PACK, P], F32, name="diff")
+        factor = keep.tile([P, PACK, P], F32, name="factor")
         neg_max = keep.tile([P, PACK], F32, name="neg_max")
         total = keep.tile([P, PACK], F32, name="total")
         inverse = keep.tile([P, PACK], F32, name="inverse")
+        targets_low = keep.tile([P, 2, REST], F32, name="targets_low")
+        targets_high = shared.tile([P, 2, REST], F32, name="targets_high", offset=0)
+        targets = [(targets_low, targets_high)[t // 2][:, t % 2, :] for t in range(PACK)]
+        y_rest = [(y_low, y_high)[t // 2][:, t % 2, :] for t in range(PACK)]
+        weights = [keep.tile([P, REST], F32, name="weights%d" % t) for t in range(PACK)]
         last = PACK - 1
 
         def scores_of(t):
             rows = slice(t * P, (t + 1) * P)
-            scores = psum.tile([P, ENTRIES], F32, name="scores%d" % t, tag="first%d" % t)
+            scores = bank(t, [ENTRIES], "scores%d" % t)
             nc.tensor.matmul_mx(
                 out=scores[:],
                 lhsT=xd_codes[:, rows].bitcast(E4M3X4),
@@ -137,11 +150,6 @@ def tile_attend_gmhm_sm_kernel(tc, xT, mT, us, wt, te, y, offs, out):
                 op1=ALU.mult,
             )
 
-        def logits_aside(t):
-            scaled = factor[:, last, :]
-            nc.scalar.activation(out=scaled, in_=scores_of(t)[:], func=ACT.Copy, scale=us_sb[:, t : t + 1])
-            nc.gpsimd.tensor_tensor(out=z[:, t, :], in0=scaled, in1=te_sb[:], op=ALU.mult)
-
         def exponentials(t):
             one = slice(t, t + 1)
             nc.vector.tensor_reduce(
@@ -154,39 +162,63 @@ def tile_attend_gmhm_sm_kernel(tc, xT, mT, us, wt, te, y, offs, out):
         def invert(lo, hi):
             nc.vector.reciprocal(out=inverse[:, lo:hi], in_=total[:, lo:hi])
 
-        def differences(t, cols):
+        def differences(t):
             nc.vector.scalar_tensor_tensor(
-                out=diff[:, t, cols],
-                in0=e[t][:, cols],
+                out=diff[:, t, :],
+                in0=e[t][:, :P],
                 scalar=inverse[:, t : t + 1],
-                in1=y_sb[:, t, cols],
+                in1=y_first[:, t, :],
                 op0=ALU.mult,
                 op1=ALU.subtract,
+            )
+
+        def weigh_targets(t):
+            nc.gpsimd.tensor_scalar(
+                out=targets[t],
+                in0=y_rest[t],
+                scalar1=row_factor[:, t : t + 1],
+                scalar2=-1.0,
+                op0=ALU.mult,
+                op1=ALU.mult,
+            )
+
+        def weigh(t):
+            nc.vector.tensor_scalar(
+                out=weights[t][:],
+                in0=e[t][:, P:],
+                scalar1=inverse[:, t : t + 1],
+                scalar2=row_factor[:, t : t + 1],
+                op0=ALU.mult,
+                op1=ALU.mult,
             )
 
         logits(0)
         logits(1)
         exponentials(0)
-        logits_aside(ASIDE)
+        for t in range(2):
+            weigh_targets(t)
+        nc.scalar.activation(out=scaled[:], in_=scores_of(ASIDE)[:], func=ACT.Copy, scale=us_sb[:, ASIDE : ASIDE + 1])
+        nc.gpsimd.tensor_tensor(out=z[:, ASIDE, :], in0=scaled[:], in1=te_sb[:], op=ALU.mult)
         logits(last)
-        for t in (1, last, ASIDE):
-            exponentials(t)
+        exponentials(1)
+        exponentials(last)
+        invert(0, 2)
+        exponentials(ASIDE)
+        for t in (last, ASIDE):
+            weigh_targets(t)
+        for t in range(PACK):
+            nc.scalar.activation(out=factor[:, t, :], in_=te_sb[:, :P], func=ACT.Copy, scale=row_factor[:, t : t + 1])
 
-        for t in range(last):
-            nc.scalar.activation(out=factor[:, t, :], in_=te_sb[:], func=ACT.Copy, scale=row_factor[:, t : t + 1])
-        nc.gpsimd.tensor_scalar(
-            out=factor[:, last, :],
-            in0=te_sb[:],
-            scalar1=row_factor[:, last:],
-            scalar2=0.0,
-            op0=ALU.mult,
-            op1=ALU.add,
-        )
+        te_turned = bank(0, [QUARTERS - 1, P], "te_turned")
+        te_cols = keep.tile([P, QUARTERS - 1], F32, name="te_cols")
+        for q in range(1, QUARTERS):
+            nc.tensor.transpose(te_turned[:, q - 1, :], te_sb[:, q * P : (q + 1) * P], identity[:])
+        nc.scalar.copy(out=te_cols[:], in_=te_turned[:, :, 0])
 
         xr_in = keep.tile([P, D, PACK], BF16, name="xr_in", tag="x_raw", align_bytes=64)
         pairs = flat(xd_in[:]).bitcast(F32).rearrange("p (n h) -> p n h", h=2)
         for h in range(2):
-            turned = psum.tile([P, PACK, P], F32, name="turned%d" % h, tag="first%d" % (2 + h))
+            turned = bank(2 + h, [PACK, P], "turned%d" % h)
             for t in range(PACK):
                 nc.tensor.transpose(turned[:, t, :], pairs[:, t * P : (t + 1) * P, h], identity[:])
             parted = turned[:].rearrange("s t p -> s (t p)").bitcast(BF16)
@@ -195,84 +227,117 @@ def tile_attend_gmhm_sm_kernel(tc, xT, mT, us, wt, te, y, offs, out):
                 j = 2 * h + member
                 nc.scalar.copy(out=xr_in[:, j * P : (j + 1) * P, :], in_=parted[:, member])
 
-        invert(0, 2)
-        differences(0, slice(0, ENTRIES))
-        invert(last, PACK)
-        differences(1, slice(0, ENTRIES))
-        invert(ASIDE, ASIDE + 1)
-        differences(last, slice(0, HALF))
-        differences(ASIDE, slice(0, HALF))
-        differences(last, slice(HALF, ENTRIES))
-
-        xr_early = keep.tile([P, EARLY * P], U32, name="xr_early", align_bytes=64)
+        xr_codes = keep.tile([P, D], U32, name="xr_codes", align_bytes=64)
         xr_scales = keep.tile([P, D], U8, name="xr_scales", align_bytes=64)
-        g_first = shared.tile([P, HALF, PACK], BF16, name="g_first", align_bytes=64, offset=G_FIRST_AT)
-        g_second = shared.tile([P, HALF, PACK], BF16, name="g_second", align_bytes=64, offset=G_SECOND_AT)
-        xr_late = shared.tile([P, D - EARLY * P], U32, name="xr_late", align_bytes=64, offset=X_LATE_AT)
-        xr_codes = [xr_early[:, j * P : (j + 1) * P] for j in range(EARLY)]
-        xr_codes.extend(xr_late[:, j * P : (j + 1) * P] for j in range(PACK - EARLY))
-        g_codes = keep.tile([P, HALF + ENTRIES], U32, name="g_codes", align_bytes=64)
-        g_scales = keep.tile([P, HALF + ENTRIES], U8, name="g_scales", align_bytes=64)
-        nc.vector.memset(g_codes[:, :HALF], 0)
-        nc.vector.memset(g_scales[:, :HALF], 0)
+        g_first = keep.tile([P, P, PACK], BF16, name="g_first", align_bytes=64)
+        g_second = keep.tile([P, P, PACK], BF16, name="g_second", align_bytes=64)
+        g_rest = keep.tile([P, HALF, PACK], BF16, name="g_rest", align_bytes=64)
+        g_codes = keep.tile([P, ENTRIES], U32, name="g_codes", align_bytes=64)
+        g_scales = keep.tile([P, ENTRIES], U8, name="g_scales", align_bytes=64)
 
-        def quantise_x(codes, lo, hi):
+        def quantise_x(lo, hi):
             nc.vector.quantize_mx(
-                out=codes.bitcast(E4M3X4), scales=xr_scales[:, lo:hi], in_=flat(xr_in[:, lo:hi, :])
-            )
-
-        def gradient(woven, lo, hi):
-            nc.vector.tensor_tensor(
-                out=woven_in_runs(woven[:]),
-                in0=in_runs(diff[:, :, lo:hi]),
-                in1=in_runs(factor[:, :, lo:hi]),
-                op=ALU.mult,
+                out=xr_codes[:, lo:hi].bitcast(E4M3X4), scales=xr_scales[:, lo:hi], in_=flat(xr_in[:, lo:hi, :])
             )
 
         def quantise_g(woven, lo, hi):
-            cols = slice(HALF + lo, HALF + hi)
-            nc.vector.quantize_mx(
-                out=g_codes[:, cols].bitcast(E5M2X4), scales=g_scales[:, cols], in_=flat(woven[:])
-            )
+            nc.vector.quantize_mx(out=g_codes[:, lo:hi].bitcast(E5M2X4), scales=g_scales[:, lo:hi], in_=flat(woven))
 
-        def product(j, first_column, bank):
+        def product(sums, j, lo, hi):
             feats = slice(j * P, (j + 1) * P)
-            cols = slice(first_column, first_column + ENTRIES)
-            sums = psum.tile([P, ENTRIES], F32, name="sums_" + bank, tag=bank)
             nc.tensor.matmul_mx(
-                out=sums[:],
-                lhsT=xr_codes[j].bitcast(E4M3X4),
+                out=sums,
+                lhsT=xr_codes[:, feats].bitcast(E4M3X4),
                 lhsT_scale=xr_scales[:, feats],
-                rhs=g_codes[:, cols].bitcast(E5M2X4),
-                rhs_scale=g_scales[:, cols],
+                rhs=g_codes[:, lo:hi].bitcast(E5M2X4),
+                rhs_scale=g_scales[:, lo:hi],
                 start=True,
                 stop=True,
             )
-            return sums
 
-        dw = keep.tile([P, PACK, ENTRIES], F32, name="dw")
         out_planes = out.rearrange("(p j) c -> p j c", j=PACK)
 
-        def scatter(j, lo, hi):
+        def scatter(j, values, lo, hi):
             listed = offsets[:, lo // LIST_ROWS : hi // LIST_ROWS]
-            nc.vector.tensor_copy(out=windows[j % WINDOWS][:].indirect(listed), in_=dw[:, j, lo:hi])
+            nc.vector.tensor_copy(out=windows[j][:].indirect(listed), in_=values)
 
-        gradient(g_first, 0, HALF)
-        quantise_x(xr_early[:], 0, EARLY * P)
-        quantise_g(g_first, 0, HALF)
-        for j in range(EARLY):
-            sums = product(j, 0, "first%d" % j)
-            nc.scalar.copy(out=dw[:, j, :HALF], in_=sums[:, HALF:])
-        differences(ASIDE, slice(HALF, ENTRIES))
-        gradient(g_second, HALF, ENTRIES)
-        quantise_x(xr_late[:], EARLY * P, D)
-        quantise_g(g_second, HALF, ENTRIES)
-        still_from = [HALF if j < EARLY else 0 for j in range(PACK)]
+        differences(0)
+        differences(1)
+        invert(last, PACK)
+        weigh(0)
+        differences(last)
+        invert(ASIDE, ASIDE + 1)
+        weigh(1)
+        differences(ASIDE)
+        weigh(last)
+        nc.vector.tensor_tensor(out=woven_in_runs(g_first[:]), in0=in_runs(diff[:]), in1=in_runs(factor[:]), op=ALU.mult)
+        quantise_x(0, HALF)
+        quantise_g(g_first[:], 0, P)
+        weigh(ASIDE)
+        quantise_x(HALF, D)
+
+        early = keep.tile([P, 2, P], F32, name="early")
+        for j in range(2):
+            sums = bank(2 + j, [P], "early%d" % j)
+            product(sums[:], j, 0, P)
+            nc.scalar.copy(out=early[:, j, :], in_=sums[:])
+            scatter(j, early[:, j, :], 0, P)
+
+        sided = [bank(number, [PACK, P], "sided%d" % number) for number in (0, 1, 4)]
+        order = (0, 1, last, ASIDE)
+        for t in order:
+            for q in range(QUARTERS - 1):
+                nc.tensor.matmul(
+                    sided[q][:, t, :], lhsT=targets[t][:, q * P : (q + 1) * P], rhs=identity[:],
+                    is_transpose=True, start=(t == order[0]), stop=False,
+                )
+        for t in order:
+            for q in range(QUARTERS - 1):
+                nc.tensor.matmul(
+                    sided[q][:, t, :], lhsT=weights[t][:, q * P : (q + 1) * P], rhs=identity[:],
+                    is_transpose=True, start=False, stop=(t == order[-1]),
+                )
+
+        def turn_back(q, woven):
+            rounded = keep.tile([P, 2, P, 2], BF16, name="rounded%d" % q)
+            nc.scalar.activation(
+                out=rounded[:],
+                in_=sided[q][:].rearrange("u (h m) s -> u h s m", m=2),
+                func=ACT.Copy,
+                scale=te_cols[:, q : q + 1],
+            )
+            back = bank(5 + q, [2, P], "back%d" % q)
+            paired = rounded[:].rearrange("u h s m -> u (h s m)").bitcast(F32)
+            for h in range(2):
+                nc.tensor.transpose(back[:, h, :], paired[:, h * P : (h + 1) * P], identity[:])
+            words = flat(woven).bitcast(F32).rearrange("s (i h) -> s i h", h=2)
+            nc.scalar.copy(out=words, in_=back[:].rearrange("s h u -> s u h"))
+
+        turn_back(0, g_second[:])
+        quantise_g(g_second[:], P, HALF)
+
+        def held_pair(number, planes, lo):
+            held = keep.tile([P, 2, P], F32, name="held%d" % number)
+            sums = bank(number, [2, P], "held_sums%d" % number)
+            for k, j in enumerate(planes):
+                product(sums[:, k, :], j, lo, lo + P)
+            nc.scalar.copy(out=held[:], in_=sums[:])
+            for k, j in enumerate(planes):
+                scatter(j, held[:, k, :], lo, lo + P)
+
+        held_pair(5, (2, 3), 0)
+        turn_back(1, g_rest[:, :P, :])
+        turn_back(2, g_rest[:, P:, :])
+        quantise_g(g_rest[:], HALF, ENTRIES)
+        held_pair(7, (0, 1), P)
+
+        dw = keep.tile([P, PACK, REST], F32, name="dw")
         for j in range(PACK):
-            sums = product(j, HALF, "second%d" % j)
-            nc.scalar.copy(out=dw[:, j, still_from[j] :], in_=sums[:, still_from[j] :])
-        for j in range(EARLY):
-            scatter(j, 0, HALF)
-        for j in range(PACK):
-            scatter(j, still_from[j], ENTRIES)
-            nc.sync.dma_start(out=out_planes[:, j, :], in_=windows[j % WINDOWS][:])
+            sums = bank((0, 1, 4, 6)[j], [REST], "late%d" % j)
+            skip = 0 if j > 1 else P
+            if j > 1:
+                product(sums[:, :P], j, P, HALF)
+            product(sums[:, P:], j, HALF, ENTRIES)
+            nc.scalar.copy(out=dw[:, j, skip:], in_=sums[:, skip:])
+            scatter(j, dw[:, j, skip:], P + skip, ENTRIES)
+            nc.sync.dma_start(out=out_planes[:, j, :], in_=windows[j][:])

@@ -82,6 +82,10 @@ def tile_attend_gmhm_sm_kernel(tc, xT, mT, us, wt, te, y, offs, out):
 
         row_factor = keep.tile([P, PACK], F32, name="row_factor")
         nc.gpsimd.tensor_tensor(out=row_factor[:], in0=wt_sb[:], in1=us_sb[:], op=ALU.mult)
+        neg_factor = keep.tile([P, 1], F32, name="neg_factor")
+        nc.gpsimd.tensor_scalar(
+            out=neg_factor[:], in0=row_factor[:, ASIDE : ASIDE + 1], scalar1=-1.0, scalar2=0.0, op0=ALU.mult, op1=ALU.add
+        )
 
         picked = keep.tile([P, PACK, ENTRIES], F32, name="picked")
         for j in range(PACK):
@@ -99,16 +103,19 @@ def tile_attend_gmhm_sm_kernel(tc, xT, mT, us, wt, te, y, offs, out):
             )
 
         xd_in = keep.tile([P, R, PACK], BF16, name="xd_in", align_bytes=64)
-        xd_codes = keep.tile([P, R], U32, name="xd_codes", align_bytes=64)
+        xd_first = keep.tile([P, P], U32, name="xd_first", align_bytes=64)
+        xd_second = shared.tile([P, P], U32, name="xd_second", align_bytes=64, offset=4096)
+        xd_rest = keep.tile([P, 2 * P], U32, name="xd_rest", align_bytes=64)
+        xd_codes = [xd_first[:], xd_second[:], xd_rest[:, :P], xd_rest[:, P:]]
         xd_scales = keep.tile([P, R], U8, name="xd_scales", align_bytes=64)
         dealt = xd_in[:].rearrange("p (t s) j -> p s j t", t=PACK)
         source = x_raw[:].rearrange("p j (s t) -> p s j t", t=PACK)
         nc.scalar.activation(out=dealt[:, : P // 2, :, :2], in_=source[:, : P // 2, :, :2], func=ACT.Copy)
         nc.vector.tensor_copy(out=dealt[:, P // 2 :, :, :2], in_=source[:, P // 2 :, :, :2])
         nc.scalar.activation(out=dealt[:, :, :, 2:], in_=source[:, :, :, 2:], func=ACT.Copy)
-        for lo, hi in ((0, P), (P, 2 * P), (2 * P, R)):
+        for codes, lo, hi in ((xd_first, 0, P), (xd_second, P, 2 * P), (xd_rest, 2 * P, R)):
             nc.vector.quantize_mx(
-                out=xd_codes[:, lo:hi].bitcast(E4M3X4), scales=xd_scales[:, lo:hi], in_=flat(xd_in[:, lo:hi, :])
+                out=codes[:].bitcast(E4M3X4), scales=xd_scales[:, lo:hi], in_=flat(xd_in[:, lo:hi, :])
             )
 
         z = keep.tile([P, PACK, ENTRIES], F32, name="z", tag="x_raw", align_bytes=64)
@@ -119,9 +126,10 @@ def tile_attend_gmhm_sm_kernel(tc, xT, mT, us, wt, te, y, offs, out):
         neg_max = keep.tile([P, PACK], F32, name="neg_max")
         total = keep.tile([P, PACK], F32, name="total")
         inverse = keep.tile([P, PACK], F32, name="inverse")
-        targets_low = keep.tile([P, 2, REST], F32, name="targets_low")
-        targets_high = shared.tile([P, 2, REST], F32, name="targets_high", offset=0)
-        targets = [(targets_low, targets_high)[t // 2][:, t % 2, :] for t in range(PACK)]
+        targets_low = shared.tile([P, 2, REST], F32, name="targets_low", offset=4096)
+        targets_aside = keep.tile([P, REST], F32, name="targets_aside")
+        targets_last = shared.tile([P, REST], F32, name="targets_last", offset=0)
+        targets = [targets_low[:, 0, :], targets_low[:, 1, :], targets_aside[:], targets_last[:]]
         y_rest = [(y_low, y_high)[t // 2][:, t % 2, :] for t in range(PACK)]
         weights = [keep.tile([P, REST], F32, name="weights%d" % t) for t in range(PACK)]
         last = PACK - 1
@@ -131,7 +139,7 @@ def tile_attend_gmhm_sm_kernel(tc, xT, mT, us, wt, te, y, offs, out):
             scores = bank(t, [ENTRIES], "scores%d" % t)
             nc.tensor.matmul_mx(
                 out=scores[:],
-                lhsT=xd_codes[:, rows].bitcast(E4M3X4),
+                lhsT=xd_codes[t].bitcast(E4M3X4),
                 lhsT_scale=xd_scales[:, rows],
                 rhs=m_codes[:].bitcast(E4M3X4),
                 rhs_scale=m_scales[:],
@@ -204,8 +212,8 @@ def tile_attend_gmhm_sm_kernel(tc, xT, mT, us, wt, te, y, offs, out):
         exponentials(last)
         invert(0, 2)
         exponentials(ASIDE)
-        for t in (last, ASIDE):
-            weigh_targets(t)
+        weigh_targets(last)
+        nc.scalar.activation(out=targets[ASIDE], in_=y_rest[ASIDE], func=ACT.Copy, scale=neg_factor[:])
         for t in range(PACK):
             nc.scalar.activation(out=factor[:, t, :], in_=te_sb[:, :P], func=ACT.Copy, scale=row_factor[:, t : t + 1])
 

@@ -80,13 +80,6 @@ def tile_attend_gmhm_sm_kernel(tc, xT, mT, us, wt, te, y, offs, out):
             nc.vector.memset(window[:], 0.0)
         nc.gpsimd.memset(windows[-1][:], 0.0)
 
-        row_factor = keep.tile([P, PACK], F32, name="row_factor")
-        nc.gpsimd.tensor_tensor(out=row_factor[:], in0=wt_sb[:], in1=us_sb[:], op=ALU.mult)
-        neg_factor = keep.tile([P, 1], F32, name="neg_factor")
-        nc.gpsimd.tensor_scalar(
-            out=neg_factor[:], in0=row_factor[:, ASIDE : ASIDE + 1], scalar1=-1.0, scalar2=0.0, op0=ALU.mult, op1=ALU.add
-        )
-
         picked = keep.tile([P, PACK, ENTRIES], F32, name="picked")
         for j in range(PACK):
             nc.vector.tensor_copy(out=picked[:, j, :], in_=memory[j][:].indirect(offsets[:]))
@@ -103,7 +96,7 @@ def tile_attend_gmhm_sm_kernel(tc, xT, mT, us, wt, te, y, offs, out):
             )
 
         xd_in = keep.tile([P, R, PACK], BF16, name="xd_in", align_bytes=64)
-        xd_first = keep.tile([P, P], U32, name="xd_first", align_bytes=64)
+        xd_first = shared.tile([P, P], U32, name="xd_first", align_bytes=64, offset=7168)
         xd_second = shared.tile([P, P], U32, name="xd_second", align_bytes=64, offset=4096)
         xd_rest = keep.tile([P, 2 * P], U32, name="xd_rest", align_bytes=64)
         xd_codes = [xd_first[:], xd_second[:], xd_rest[:, :P], xd_rest[:, P:]]
@@ -167,8 +160,8 @@ def tile_attend_gmhm_sm_kernel(tc, xT, mT, us, wt, te, y, offs, out):
                 out=e[t][:], in_=z[:, t, :], func=ACT.Exp, bias=neg_max[:, one], accum_out=total[:, one]
             )
 
-        def invert(lo, hi):
-            nc.vector.reciprocal(out=inverse[:, lo:hi], in_=total[:, lo:hi])
+        def invert(tiles):
+            nc.vector.reciprocal(out=inverse[:, tiles], in_=total[:, tiles])
 
         def differences(t):
             nc.vector.scalar_tensor_tensor(
@@ -201,6 +194,13 @@ def tile_attend_gmhm_sm_kernel(tc, xT, mT, us, wt, te, y, offs, out):
             )
 
         logits(0)
+        row_factor = shared.tile([P, PACK], F32, name="row_factor", offset=7168)
+        nc.gpsimd.tensor_tensor(out=row_factor[:], in0=wt_sb[:], in1=us_sb[:], op=ALU.mult)
+        neg_factor = keep.tile([P, 1], F32, name="neg_factor")
+        nc.gpsimd.tensor_scalar(
+            out=neg_factor[:], in0=row_factor[:, ASIDE : ASIDE + 1], scalar1=-1.0, scalar2=0.0, op0=ALU.mult, op1=ALU.add
+        )
+
         logits(1)
         exponentials(0)
         for t in range(2):
@@ -210,7 +210,7 @@ def tile_attend_gmhm_sm_kernel(tc, xT, mT, us, wt, te, y, offs, out):
         logits(last)
         exponentials(1)
         exponentials(last)
-        invert(0, 2)
+        invert(slice(0, 1))
         exponentials(ASIDE)
         weigh_targets(last)
         nc.scalar.activation(out=targets[ASIDE], in_=y_rest[ASIDE], func=ACT.Copy, scale=neg_factor[:])
@@ -270,17 +270,16 @@ def tile_attend_gmhm_sm_kernel(tc, xT, mT, us, wt, te, y, offs, out):
             nc.vector.tensor_copy(out=windows[j][:].indirect(listed), in_=values)
 
         differences(0)
-        differences(1)
-        invert(last, PACK)
+        invert(slice(1, PACK, 2))
         weigh(0)
-        differences(last)
-        invert(ASIDE, ASIDE + 1)
+        invert(slice(ASIDE, ASIDE + 1))
+        for t in (1, last, ASIDE):
+            differences(t)
         weigh(1)
-        differences(ASIDE)
-        weigh(last)
         nc.vector.tensor_tensor(out=woven_in_runs(g_first[:]), in0=in_runs(diff[:]), in1=in_runs(factor[:]), op=ALU.mult)
         quantise_x(0, HALF)
         quantise_g(g_first[:], 0, P)
+        weigh(last)
         weigh(ASIDE)
         quantise_x(HALF, D)
 
@@ -306,7 +305,7 @@ def tile_attend_gmhm_sm_kernel(tc, xT, mT, us, wt, te, y, offs, out):
                     is_transpose=True, start=False, stop=(t == order[-1]),
                 )
 
-        def turn_back(q, woven):
+        def scale_and_turn(q):
             rounded = keep.tile([P, 2, P, 2], BF16, name="rounded%d" % q)
             nc.scalar.activation(
                 out=rounded[:],
@@ -314,34 +313,39 @@ def tile_attend_gmhm_sm_kernel(tc, xT, mT, us, wt, te, y, offs, out):
                 func=ACT.Copy,
                 scale=te_cols[:, q : q + 1],
             )
-            back = bank(5 + q, [2, P], "back%d" % q)
             paired = rounded[:].rearrange("u h s m -> u (h s m)").bitcast(F32)
             for h in range(2):
-                nc.tensor.transpose(back[:, h, :], paired[:, h * P : (h + 1) * P], identity[:])
-            words = flat(woven).bitcast(F32).rearrange("s (i h) -> s i h", h=2)
-            nc.scalar.copy(out=words, in_=back[:].rearrange("s h u -> s u h"))
+                nc.tensor.transpose(back[q][:, h, :], paired[:, h * P : (h + 1) * P], identity[:])
 
-        turn_back(0, g_second[:])
-        quantise_g(g_second[:], P, HALF)
+        def bring_back(q, woven):
+            words = flat(woven).bitcast(F32).rearrange("s (u h) -> s u h", h=2)
+            nc.scalar.copy(out=words, in_=back[q][:].rearrange("s h u -> s u h"))
 
-        def held_pair(number, planes, lo):
-            held = keep.tile([P, 2, P], F32, name="held%d" % number)
-            sums = bank(number, [2, P], "held_sums%d" % number)
+        def short_products(number, planes, lo):
+            values = keep.tile([P, len(planes), P], F32, name="values%d" % number)
+            sums = bank(number, [len(planes), P], "short%d" % number)
             for k, j in enumerate(planes):
                 product(sums[:, k, :], j, lo, lo + P)
-            nc.scalar.copy(out=held[:], in_=sums[:])
+            nc.scalar.copy(out=values[:], in_=sums[:])
             for k, j in enumerate(planes):
-                scatter(j, held[:, k, :], lo, lo + P)
+                scatter(j, values[:, k, :], lo, lo + P)
 
-        held_pair(5, (2, 3), 0)
-        turn_back(1, g_rest[:, :P, :])
-        turn_back(2, g_rest[:, P:, :])
+        back = [bank(5 + q, [2, P], "back%d" % q) for q in range(QUARTERS - 1)]
+        scale_and_turn(0)
+        bring_back(0, g_second[:])
+        quantise_g(g_second[:], P, HALF)
+        short_products(0, (2,), 0)
+        scale_and_turn(1)
+        scale_and_turn(2)
+        short_products(1, (last,), 0)
+        bring_back(1, g_rest[:, :P, :])
+        bring_back(2, g_rest[:, P:, :])
         quantise_g(g_rest[:], HALF, ENTRIES)
-        held_pair(7, (0, 1), P)
+        short_products(4, (0, 1), P)
 
         dw = keep.tile([P, PACK, REST], F32, name="dw")
         for j in range(PACK):
-            sums = bank((0, 1, 4, 6)[j], [REST], "late%d" % j)
+            sums = bank((3, 2, 7, 4)[j], [REST], "late%d" % j)
             skip = 0 if j > 1 else P
             if j > 1:
                 product(sums[:, :P], j, P, HALF)

from contextlib import ExitStack

import concourse.mybir as mybir
from concourse.masks import make_identity

D, R, ENTRIES, PLACES = 512, 512, 512, 2048
FLOPS = 2 * 2 * D * R * ENTRIES

F32 = mybir.dt.float32
BF16 = mybir.dt.bfloat16
U32 = mybir.dt.uint32
U16 = mybir.dt.uint16
U8 = mybir.dt.uint8
E4M3X4 = mybir.dt.float8_e4m3fn_x4
E5M2X4 = mybir.dt.float8_e5m2_x4
ALU = mybir.AluOpType
ACT = mybir.ActivationFunctionType

P = 128
PACK = 4
RUN = 4
HALF = ENTRIES // 2
LIST_ROWS = 16
ASIDE = 2
SCALAR_FROM = 336
QUARTERS = ENTRIES // P
REST = ENTRIES - P


def in_runs(planes):
    return planes.rearrange("p t (c i) -> p c t i", i=RUN)


def woven_in_runs(woven):
    return woven.rearrange("p (c i) t -> p c t i", i=RUN)


def flat(woven):
    return woven.rearrange("p n t -> p (n t)")


def tile_attend_gmhm_sm_kernel(tc, xT, mT, us, wt, te, y, offs, out):
    nc = tc.nc
    with ExitStack() as ctx:
        keep = ctx.enter_context(tc.tile_pool(name="keep", bufs=1))
        shared = ctx.enter_context(tc.tile_pool(name="shared", bufs=1))
        psum = ctx.enter_context(tc.psum_pool(name="psum", bufs=1))

        def bank(number, shape, name):
            return psum.tile([P] + shape, F32, name=name, tag="bank%d" % number)

        offsets = keep.tile([P, ENTRIES // LIST_ROWS], U16, name="offsets")
        x_raw = keep.tile([P, PACK, R], F32, name="x_raw", tag="x_raw", align_bytes=64)
        memory = [keep.tile([P, PLACES], F32, name="memory%d" % j) for j in range(PACK)]
        us_sb = keep.tile([P, PACK], F32, name="us_sb")
        wt_sb = keep.tile([P, PACK], F32, name="wt_sb")
        te_sb = keep.tile([P, ENTRIES], F32, name="te_sb")
        y_first = keep.tile([P, PACK, P], F32, name="y_first")
        y_low = keep.tile([P, 2, REST], F32, name="y_low")
        y_high = keep.tile([P, 2, REST], F32, name="y_high")

        m_planes = mT.rearrange("(p j) c -> p j c", j=PACK)
        y_tiles = y.rearrange("(s t) i -> s t i", t=PACK)
        nc.sync.dma_start(out=memory[0][:], in_=m_planes[:, 0, :])
        nc.sync.dma_start(offsets[:], offs)
        for j in range(1, PACK):
            nc.sync.dma_start(out=memory[j][:], in_=m_planes[:, j, :])
        nc.sync.dma_start(out=x_raw[:], in_=xT.rearrange("(p j) r -> p j r", j=PACK))
        nc.sync.dma_start(out=us_sb[:], in_=us.rearrange("(s t) o -> s (t o)", t=PACK))
        nc.sync.dma_start(out=wt_sb[:], in_=wt.rearrange("(s t) o -> s (t o)", t=PACK))
        nc.sync.dma_start(out=te_sb[:], in_=te)
        nc.sync.dma_start(out=y_first[:], in_=y_tiles[:, :, :P])
        nc.sync.dma_start(out=y_low[:], in_=y_tiles[:, :2, P:])
        nc.sync.dma_start(out=y_high[:], in_=y_tiles[:, 2:, P:])

        windows = [keep.tile([P, PLACES], F32, name="window%d" % w) for w in range(PACK)]
        identity = keep.tile([P, P], F32, name="identity")
        make_identity(nc, identity[:])
        for window in windows[:-1]:
            nc.vector.memset(window[:], 0.0)
        nc.gpsimd.memset(windows[-1][:], 0.0)

        picked = keep.tile([P, PACK, ENTRIES], F32, name="picked")
        for j in range(PACK):
            nc.vector.tensor_copy(out=picked[:, j, :], in_=memory[j][:].indirect(offsets[:]))
        m_in = keep.tile([P, ENTRIES, PACK], BF16, name="m_in", align_bytes=64)
        m_codes = keep.tile([P, ENTRIES], U32, name="m_codes", align_bytes=64)
        m_scales = keep.tile([P, ENTRIES], U8, name="m_scales", align_bytes=64)
        for lo, hi in ((0, HALF), (HALF, SCALAR_FROM)):
            nc.vector.tensor_copy(out=woven_in_runs(m_in[:, lo:hi, :]), in_=in_runs(picked[:, :, lo:hi]))
        nc.scalar.copy(out=woven_in_runs(m_in[:, SCALAR_FROM:, :]), in_=in_runs(picked[:, :, SCALAR_FROM:]))
        for lo in (0, HALF):
            cols = slice(lo, lo + HALF)
            nc.vector.quantize_mx(
                out=m_codes[:, cols].bitcast(E4M3X4), scales=m_scales[:, cols], in_=flat(m_in[:, cols, :])
            )

        xd_in = keep.tile([P, R, PACK], BF16, name="xd_in", align_bytes=64)
        xd_first = shared.tile([P, P], U32, name="xd_first", align_bytes=64, offset=7168)
        xd_second = shared.tile([P, P], U32, name="xd_second", align_bytes=64, offset=4096)
        xd_rest = keep.tile([P, 2 * P], U32, name="xd_rest", align_bytes=64)
        xd_codes = [xd_first[:], xd_second[:], xd_rest[:, :P], xd_rest[:, P:]]
        xd_scales = keep.tile([P, R], U8, name="xd_scales", align_bytes=64)
        dealt = xd_in[:].rearrange("p (t s) j -> p s j t", t=PACK)
        source = x_raw[:].rearrange("p j (s t) -> p s j t", t=PACK)
        nc.scalar.activation(out=dealt[:, : P // 2, :, :2], in_=source[:, : P // 2, :, :2], func=ACT.Copy)
        nc.vector.tensor_copy(out=dealt[:, P // 2 :, :, :2], in_=source[:, P // 2 :, :, :2])
        nc.scalar.activation(out=dealt[:, :, :, 2:], in_=source[:, :, :, 2:], func=ACT.Copy)
        for codes, lo, hi in ((xd_first, 0, P), (xd_second, P, 2 * P), (xd_rest, 2 * P, R)):
            nc.vector.quantize_mx(
                out=codes[:].bitcast(E4M3X4), scales=xd_scales[:, lo:hi], in_=flat(xd_in[:, lo:hi, :])
            )

        z = keep.tile([P, PACK, ENTRIES], F32, name="z", tag="x_raw", align_bytes=64)
        e = [keep.tile([P, ENTRIES], F32, name="e%d" % t) for t in range(PACK)]
        scaled = shared.tile([P, ENTRIES], F32, name="scaled", offset=0)
        diff = keep.tile([P, PACK, P], F32, name="diff")
        factor = keep.tile([P, PACK, P], F32, name="factor")
        neg_max = keep.tile([P, PACK], F32, name="neg_max")
        total = keep.tile([P, PACK], F32, name="total")
        inverse = keep.tile([P, PACK], F32, name="inverse")
        targets_low = shared.tile([P, 2, REST], F32, name="targets_low", offset=4096)
        targets_aside = keep.tile([P, REST], F32, name="targets_aside")
        targets_last = shared.tile([P, REST], F32, name="targets_last", offset=0)
        targets = [targets_low[:, 0, :], targets_low[:, 1, :], targets_aside[:], targets_last[:]]
        y_rest = [(y_low, y_high)[t // 2][:, t % 2, :] for t in range(PACK)]
        weights = [keep.tile([P, REST], F32, name="weights%d" % t) for t in range(PACK)]
        last = PACK - 1

        def scores_of(t):
            rows = slice(t * P, (t + 1) * P)
            scores = bank(t, [ENTRIES], "scores%d" % t)
            nc.tensor.matmul_mx(
                out=scores[:],
                lhsT=xd_codes[t].bitcast(E4M3X4),
                lhsT_scale=xd_scales[:, rows],
                rhs=m_codes[:].bitcast(E4M3X4),
                rhs_scale=m_scales[:],
                start=True,
                stop=True,
            )
            return scores

        def logits(t):
            nc.vector.scalar_tensor_tensor(
                out=z[:, t, :],
                in0=scores_of(t)[:],
                scalar=us_sb[:, t : t + 1],
                in1=te_sb[:],
                op0=ALU.mult,
                op1=ALU.mult,
            )

        def exponentials(t):
            one = slice(t, t + 1)
            nc.vector.tensor_reduce(
                out=neg_max[:, one], in_=z[:, t, :], axis=mybir.AxisListType.X, op=ALU.max, negate=True
            )
            nc.scalar.activation(
                out=e[t][:], in_=z[:, t, :], func=ACT.Exp, bias=neg_max[:, one], accum_out=total[:, one]
            )

        def invert(tiles):
            nc.vector.reciprocal(out=inverse[:, tiles], in_=total[:, tiles])

        def differences(t):
            nc.vector.scalar_tensor_tensor(
                out=diff[:, t, :],
                in0=e[t][:, :P],
                scalar=inverse[:, t : t + 1],
                in1=y_first[:, t, :],
                op0=ALU.mult,
                op1=ALU.subtract,
            )

        def weigh_targets(t):
            nc.gpsimd.tensor_scalar(
                out=targets[t],
                in0=y_rest[t],
                scalar1=row_factor[:, t : t + 1],
                scalar2=-1.0,
                op0=ALU.mult,
                op1=ALU.mult,
            )

        def weigh(t):
            nc.vector.tensor_scalar(
                out=weights[t][:],
                in0=e[t][:, P:],
                scalar1=inverse[:, t : t + 1],
                scalar2=row_factor[:, t : t + 1],
                op0=ALU.mult,
                op1=ALU.mult,
            )

        logits(0)
        row_factor = shared.tile([P, PACK], F32, name="row_factor", offset=7168)
        nc.gpsimd.tensor_tensor(out=row_factor[:], in0=wt_sb[:], in1=us_sb[:], op=ALU.mult)
        neg_factor = keep.tile([P, 1], F32, name="neg_factor")
        nc.gpsimd.tensor_scalar(
            out=neg_factor[:], in0=row_factor[:, ASIDE : ASIDE + 1], scalar1=-1.0, scalar2=0.0, op0=ALU.mult, op1=ALU.add
        )

        logits(1)
        exponentials(0)
        for t in range(2):
            weigh_targets(t)
        nc.scalar.activation(out=scaled[:], in_=scores_of(ASIDE)[:], func=ACT.Copy, scale=us_sb[:, ASIDE : ASIDE + 1])
        nc.gpsimd.tensor_tensor(out=z[:, ASIDE, :], in0=scaled[:], in1=te_sb[:], op=ALU.mult)
        logits(last)
        exponentials(1)
        exponentials(last)
        invert(slice(0, 1))
        exponentials(ASIDE)
        weigh_targets(last)
        nc.scalar.activation(out=targets[ASIDE], in_=y_rest[ASIDE], func=ACT.Copy, scale=neg_factor[:])
        for t in range(PACK):
            nc.scalar.activation(out=factor[:, t, :], in_=te_sb[:, :P], func=ACT.Copy, scale=row_factor[:, t : t + 1])

        te_turned = bank(0, [QUARTERS - 1, P], "te_turned")
        te_cols = keep.tile([P, QUARTERS - 1], F32, name="te_cols")
        for q in range(1, QUARTERS):
            nc.tensor.transpose(te_turned[:, q - 1, :], te_sb[:, q * P : (q + 1) * P], identity[:])
        nc.scalar.copy(out=te_cols[:], in_=te_turned[:, :, 0])

        xr_in = keep.tile([P, D, PACK], BF16, name="xr_in", tag="x_raw", align_bytes=64)
        pairs = flat(xd_in[:]).bitcast(F32).rearrange("p (n h) -> p n h", h=2)
        for h in range(2):
            turned = bank(2 + h, [PACK, P], "turned%d" % h)
            for t in range(PACK):
                nc.tensor.transpose(turned[:, t, :], pairs[:, t * P : (t + 1) * P, h], identity[:])
            parted = turned[:].rearrange("s t p -> s (t p)").bitcast(BF16)
            parted = parted.rearrange("s (t p m) -> s m p t", t=PACK, m=2)
            for member in range(2):
                j = 2 * h + member
                nc.scalar.copy(out=xr_in[:, j * P : (j + 1) * P, :], in_=parted[:, member])

        xr_codes = keep.tile([P, D], U32, name="xr_codes", align_bytes=64)
        xr_scales = keep.tile([P, D], U8, name="xr_scales", align_bytes=64)
        g_first = keep.tile([P, P, PACK], BF16, name="g_first", align_bytes=64)
        g_second = keep.tile([P, P, PACK], BF16, name="g_second", align_bytes=64)
        g_rest = keep.tile([P, HALF, PACK], BF16, name="g_rest", align_bytes=64)
        g_codes = keep.tile([P, ENTRIES], U32, name="g_codes", align_bytes=64)
        g_scales = keep.tile([P, ENTRIES], U8, name="g_scales", align_bytes=64)

        def quantise_x(lo, hi):
            nc.vector.quantize_mx(
                out=xr_codes[:, lo:hi].bitcast(E4M3X4), scales=xr_scales[:, lo:hi], in_=flat(xr_in[:, lo:hi, :])
            )

        def quantise_g(woven, lo, hi):
            nc.vector.quantize_mx(out=g_codes[:, lo:hi].bitcast(E5M2X4), scales=g_scales[:, lo:hi], in_=flat(woven))

        def product(sums, j, lo, hi):
            feats = slice(j * P, (j + 1) * P)
            nc.tensor.matmul_mx(
                out=sums,
                lhsT=xr_codes[:, feats].bitcast(E4M3X4),
                lhsT_scale=xr_scales[:, feats],
                rhs=g_codes[:, lo:hi].bitcast(E5M2X4),
                rhs_scale=g_scales[:, lo:hi],
                start=True,
                stop=True,
            )

        out_planes = out.rearrange("(p j) c -> p j c", j=PACK)

        def scatter(j, values, lo, hi):
            listed = offsets[:, lo // LIST_ROWS : hi // LIST_ROWS]
            nc.vector.tensor_copy(out=windows[j][:].indirect(listed), in_=values)

        differences(0)
        invert(slice(1, PACK, 2))
        weigh(0)
        invert(slice(ASIDE, ASIDE + 1))
        for t in (1, last, ASIDE):
            differences(t)
        weigh(1)
        nc.vector.tensor_tensor(out=woven_in_runs(g_first[:]), in0=in_runs(diff[:]), in1=in_runs(factor[:]), op=ALU.mult)
        quantise_x(0, HALF)
        quantise_g(g_first[:], 0, P)
        weigh(last)
        weigh(ASIDE)
        quantise_x(HALF, D)

        early = keep.tile([P, 2, P], F32, name="early")
        for j in range(2):
            sums = bank(2 + j, [P], "early%d" % j)
            product(sums[:], j, 0, P)
            nc.scalar.copy(out=early[:, j, :], in_=sums[:])
            scatter(j, early[:, j, :], 0, P)

        sided = [bank(number, [PACK, P], "sided%d" % number) for number in (0, 1, 4)]
        order = (0, 1, last, ASIDE)
        for t in order:
            for q in range(QUARTERS - 1):
                nc.tensor.matmul(
                    sided[q][:, t, :], lhsT=targets[t][:, q * P : (q + 1) * P], rhs=identity[:],
                    is_transpose=True, start=(t == order[0]), stop=False,
                )
        for t in order:
            for q in range(QUARTERS - 1):
                nc.tensor.matmul(
                    sided[q][:, t, :], lhsT=weights[t][:, q * P : (q + 1) * P], rhs=identity[:],
                    is_transpose=True, start=False, stop=(t == order[-1]),
                )

        def scale_and_turn(q):
            rounded = keep.tile([P, 2, P, 2], BF16, name="rounded%d" % q)
            nc.scalar.activation(
                out=rounded[:],
                in_=sided[q][:].rearrange("u (h m) s -> u h s m", m=2),
                func=ACT.Copy,
                scale=te_cols[:, q : q + 1],
            )
            paired = rounded[:].rearrange("u h s m -> u (h s m)").bitcast(F32)
            for h in range(2):
                nc.tensor.transpose(back[q][:, h, :], paired[:, h * P : (h + 1) * P], identity[:])

        def bring_back(q, woven):
            words = flat(woven).bitcast(F32).rearrange("s (u h) -> s u h", h=2)
            nc.scalar.copy(out=words, in_=back[q][:].rearrange("s h u -> s u h"))

        def short_products(number, planes, lo):
            values = keep.tile([P, len(planes), P], F32, name="values%d" % number)
            sums = bank(number, [len(planes), P], "short%d" % number)
            for k, j in enumerate(planes):
                product(sums[:, k, :], j, lo, lo + P)
            nc.scalar.copy(out=values[:], in_=sums[:])
            for k, j in enumerate(planes):
                scatter(j, values[:, k, :], lo, lo + P)

        back = [bank(5 + q, [2, P], "back%d" % q) for q in range(QUARTERS - 1)]
        scale_and_turn(0)
        bring_back(0, g_second[:])
        quantise_g(g_second[:], P, HALF)
        short_products(0, (2,), 0)
        scale_and_turn(1)
        scale_and_turn(2)
        short_products(1, (last,), 0)
        bring_back(1, g_rest[:, :P, :])
        bring_back(2, g_rest[:, P:, :])
        quantise_g(g_rest[:], HALF, ENTRIES)
        short_products(4, (0, 1), P)

        dw = keep.tile([P, PACK, REST], F32, name="dw")
        for j in range(PACK):
            sums = bank((3, 2, 7, 4)[j], [REST], "late%d" % j)
            skip = 0 if j > 1 else P
            if j > 1:
                product(sums[:, :P], j, P, HALF)
            product(sums[:, P:], j, HALF, ENTRIES)
            nc.scalar.copy(out=dw[:, j, skip:], in_=sums[:, skip:])
            scatter(j, dw[:, j, skip:], P + skip, ENTRIES)
            nc.sync.dma_start(out=out_planes[:, j, :], in_=windows[j][:])
